import numpy as np
import ml_dtypes


def mxq(x, axis, fmt="e4m3"):
    dtype, down = {"e4m3": (ml_dtypes.float8_e4m3fn, 7), "e5m2": (ml_dtypes.float8_e5m2, 14)}[fmt]
    v = np.moveaxis(np.asarray(x, np.float32).astype(ml_dtypes.bfloat16).astype(np.float64), axis, -1)
    blocks = v.reshape(v.shape[:-1] + (-1, 32))
    amax = np.abs(blocks).max(-1, keepdims=True)
    byte = np.maximum(np.where(amax > 0, np.frexp(amax)[1] - 1 + 127, 0) - down, 1)
    scale = np.exp2(byte - 127.0)
    codes = (blocks / scale).astype(np.float32).astype(dtype).astype(np.float64)
    return np.moveaxis((codes * scale).reshape(v.shape), -1, axis)


WIDE = False


def mx_kscale(k):
    if not WIDE:
        return np.ones(k)
    levels = np.array([10, -10, 5, -5, 0])
    if k % 512:
        return np.exp2(np.random.permutation(np.resize(levels, k // 32))).repeat(32)
    a = np.empty((k // 512, 16))
    for p in range(k // 512):
        a[p, :8] = np.random.permutation(np.resize(levels, 8))
        for g in range(8):
            far = levels[np.abs(levels - a[p, g]) >= 10]
            a[p, g + 8] = far[np.random.randint(len(far))]
    return np.exp2(a.ravel()).repeat(32)


BF16 = ml_dtypes.bfloat16


def bf(x):
    return np.asarray(x, np.float32).astype(BF16)


def f64(x):
    return np.asarray(x).astype(np.float64)


E2M1 = np.array([0.0, 0.5, 1.0, 1.5, 2.0, 3.0, 4.0, 6.0, -0.0, -0.5, -1.0, -1.5, -2.0, -3.0, -4.0, -6.0])


def pack_weight(w, fmt):
    k, n = w.shape
    w = f64(bf(w)).reshape(k // 32, 32, n)
    amax = np.abs(w).max(1)
    if fmt == "e4m3":
        byte = np.frexp(amax)[1] - 1 + 127 - 7
    else:
        mant, ex = np.frexp(amax / 6.0)
        byte = np.where(mant > 0.5, ex, ex - 1) + 127
    byte = np.clip(np.where(amax > 0, byte, 1), 1, 254)
    scaled = (w * np.exp2(127.0 - byte)[:, None, :]).reshape(k, n).astype(np.float32)
    by_word = np.ascontiguousarray(scaled.reshape(k // 512, 128, 4, n).transpose(0, 1, 3, 2))
    if fmt == "e4m3":
        words = by_word.astype(ml_dtypes.float8_e4m3fn).view(np.uint8)
    else:
        c = by_word.astype(ml_dtypes.float4_e2m1fn).view(np.uint8) & 0xF
        words = c[..., 0::2] | (c[..., 1::2] << 4)
    return np.ascontiguousarray(words), np.ascontiguousarray(byte.astype(np.uint8).reshape(k // 512, 16, n))


def unpack_weight(words, scales, fmt):
    g, p, n, _ = words.shape
    if fmt == "e4m3":
        vals = np.ascontiguousarray(words).view(ml_dtypes.float8_e4m3fn).astype(np.float64)
    else:
        nib = np.empty((g, p, n, 4), np.uint8)
        nib[..., 0::2] = words & 0xF
        nib[..., 1::2] = words >> 4
        vals = E2M1[nib]
    vals = vals * np.repeat(np.exp2(scales.astype(np.float64) - 127.0), 8, axis=1)[..., None]
    return vals.transpose(0, 1, 3, 2).reshape(g * 512, n)
def pack4(w):
    words, scales = pack_weight(w, "e2m1")
    return words.reshape(words.shape[0], 128, -1), scales


def unpack4(words, scales):
    return unpack_weight(words.reshape(words.shape[0], 128, -1, 2), scales, "e2m1")


E4M3FN = np.array([(-1.0 if i & 128 else 1.0) * ((1.0 + (i & 7) / 8.0) * 2.0 ** (((i >> 3) & 15) - 7) if i & 120 else (i & 7) * 2.0 ** -9) for i in range(256)])


def e4m3fn_bytes(y):
    return np.clip(np.asarray(y, np.float64), -448.0, 448.0).astype(np.float32).astype(ml_dtypes.float8_e4m3fn).view(np.uint8)


def e4m3fn_values(b):
    return E4M3FN[b]

def planes(Y):
    n, m = Y.shape
    b = f64(bf(Y)).reshape(n // 32, 32, m)
    amax = np.abs(b).max(1)
    byte = np.clip(np.where(amax > 0, np.frexp(amax)[1] - 1 + 127 - 7, 1), 1, 254)
    codes = (b * np.exp2(127.0 - byte)[:, None, :]).reshape(n, m).astype(np.float32).astype(ml_dtypes.float8_e4m3fn).view(np.uint8)
    words = codes.reshape(n // 512, 128, 4, m).transpose(0, 1, 3, 2)
    return np.ascontiguousarray(words), np.ascontiguousarray(byte.astype(np.uint8).reshape(n // 512, 16, m))


T, K, N, B = 1280, 1536, 1024, 128

def setup_inputs():
    s = mx_kscale(K)
    strength = np.exp(0.3 * np.random.randn(T, 1))
    X = strength * np.random.randn(T, K) * s[None, :]
    X_scale = (np.abs(X).reshape(T, K // B, B).max(axis=2) / 448.0).astype(np.float32)
    X_bytes = e4m3fn_bytes(X / np.repeat(f64(X_scale), B, axis=1))
    size = np.exp(0.8 * np.random.randn(1, N))
    phase = np.random.uniform(-3.0, 3.0, (K, N))
    Wi = size * np.cos(phase) * np.sqrt(2.0 / K) / s[:, None]
    Wq = size * np.sin(phase) * np.sqrt(2.0 / K) / s[:, None]
    Wi_words, Wi_scales = pack4(Wi)
    Wq_words, Wq_scales = pack4(Wq)
    thr = bf(0.6 * size * np.exp(0.2 * np.random.randn(1, N)))
    return {"X_bytes": X_bytes, "X_scale": X_scale,
            "Wi_words": Wi_words, "Wi_scales": Wi_scales,
            "Wq_words": Wq_words, "Wq_scales": Wq_scales, "thr": thr}

def reference(X_bytes, X_scale, Wi_words, Wi_scales, Wq_words, Wq_scales, thr):
    X = e4m3fn_values(X_bytes) * np.repeat(f64(X_scale), B, axis=1)
    Xm = mxq(X, 1, "e4m3")
    I = Xm @ unpack4(Wi_words, Wi_scales)
    Q = Xm @ unpack4(Wq_words, Wq_scales)
    y = np.sqrt(I * I + Q * Q) - f64(thr)
    words, scales = planes(y.T)
    return y, words, scales

@@ -1,0 +1,386 @@
+from contextlib import ExitStack
+
+import concourse.mybir as mybir
+from concourse.masks import make_identity
+
+T, K, N = 1280, 1536, 1024
+FLOPS = 2 * 2 * T * K * N
+
+F32 = mybir.dt.float32
+BF16 = mybir.dt.bfloat16
+I32 = mybir.dt.int32
+U32 = mybir.dt.uint32
+U8 = mybir.dt.uint8
+FP8 = mybir.dt.float8_e4m3fn
+FP8X4 = mybir.dt.float8_e4m3fn_x4
+FP4X4 = mybir.dt.float4_e2m1fn_x4
+ALU = mybir.AluOpType
+ACT = mybir.ActivationFunctionType
+
+P = 128
+KPASS = 512
+PASSES = K // KPASS
+HALF = 512
+HALVES = N // HALF
+TILES = T // P
+UNITS = TILES * HALVES
+BLOCK = 128
+BLOCKS = K // BLOCK
+BANKS = 8
+X_LOADS = ((0, 1), (1, 3), (3, 5), (5, 10))
+EARLY_SCALE_TILES = 8
+Y_LAG = 3
+DOUBLE_RUNS = 0
+SWAP = 1
+COPIES = 2
+WIDENS = (2, 2)
+V_REST = 99
+V_FIRST = 7
+V_Y_END = 16
+S_TILE = 99
+ROOT_FIRST = 0
+TURN1_LATE = 0
+HEAD_WIDE = 3
+PIECES = 2
+V_Y = 99
+X_POS = 0
+
+
+def tile_radar_iq_envelope_planes_b2_kernel(
+    tc, X_bytes, X_scale, Wi_words, Wi_scales, Wq_words, Wq_scales, thr, out_0, out_1, out_2
+):
+    nc = tc.nc
+    with ExitStack() as ctx:
+        keep = ctx.enter_context(tc.tile_pool(name="keep", bufs=1))
+        work = ctx.enter_context(tc.tile_pool(name="work", bufs=3))
+        psum = ctx.enter_context(tc.psum_pool(name="psum", bufs=1))
+        ctx.enter_context(tc.manual_schedule())
+
+        free_banks = list(range(BANKS))
+        bank_number = {}
+
+        def next_bank(key):
+            n = free_banks[0]
+            free_banks.remove(n)
+            bank_number[key] = n
+            return psum.tile([P, HALF], F32, name="bank%d" % n, tag="bank%d" % n)
+
+        def emptied(key):
+            free_banks.append(bank_number[key])
+
+        ident = keep.tile([P, P], F32, name="ident")
+        make_identity(nc, ident[:])
+        warm = keep.tile([P, 2], F32, name="warm")
+        w_scales = []
+        for name in ("wi_scales", "wq_scales"):
+            plane = keep.tile([P, PASSES * N], U8, name=name, align_bytes=64)
+            nc.vector.memset(plane[:].bitcast(I32), 0)
+            w_scales.append(plane)
+        nc.vector.memset(warm[:, 0:1], 1.0)
+        nc.scalar.activation(out=warm[:, 1:2], in_=warm[:, 0:1], func=ACT.Sqrt)
+
+        x_raw = {}
+
+        def load_x(first, last):
+            raw = keep.tile([P, last - first, K], U8, name="x_raw%d" % first)
+            nc.sync.dma_start(out=raw[:], in_=X_bytes[first * P : last * P, :].rearrange("(j p) k -> p j k", p=P))
+            for j in range(first, last):
+                x_raw[j] = raw[:, j - first, :]
+
+        def load_w_scales(part):
+            src = (Wi_scales, Wq_scales)[part]
+            for q in range(4):
+                nc.sync.dma_start(
+                    out=w_scales[part][32 * q : 32 * q + 4, :].bitcast(I32).rearrange("r (g n) -> r g n", g=PASSES),
+                    in_=src[:, 4 * q : 4 * q + 4, :].bitcast(I32).rearrange("g r n -> r g n"),
+                )
+
+        w_words = {}
+
+        def load_w_words(part, h):
+            src = (Wi_words, Wq_words)[part]
+            words = keep.tile([P, PASSES, 2 * HALF], U8, name="w_words%d%d" % (part, h), align_bytes=64)
+            nc.sync.dma_start(out=words[:], in_=src[:, :, 2 * HALF * h : 2 * HALF * (h + 1)].rearrange("g p b -> p g b"))
+            w_words[part, h] = words
+
+        load_x(*X_LOADS[0])
+        x_scale = keep.tile([P, TILES, BLOCKS], F32, name="x_scale")
+        nc.sync.dma_start(out=x_scale[:], in_=X_scale.rearrange("(j p) c -> p j c", p=P))
+        load_x(*X_LOADS[1])
+        load_w_scales(0)
+        load_w_words(0, 0)
+        load_w_scales(1)
+        load_w_words(1, 0)
+        if X_POS == 0:
+            load_x(*X_LOADS[2])
+        load_w_words(0, 1)
+        load_w_words(1, 1)
+        if X_POS == 1:
+            load_x(*X_LOADS[2])
+        thr_rows = keep.tile([P, N], BF16, name="thr_rows")
+        nc.sync.dma_start(out=thr_rows[:], in_=thr.rearrange("o n -> (o n)").partition_broadcast(P))
+        load_x(*X_LOADS[3])
+
+        x_wide, x_bank, x_turned, x_codes, x_scales = {}, {}, {}, {}, {}
+
+        def widen(j, g):
+            wide = work.tile([P, KPASS], BF16, name="x_wide", tag="x_wide", bufs=15)
+            sorted_view = wide[:].rearrange("p (u r e) -> p r u e", u=2, e=2)
+            for q in range(4):
+                b = 4 * g + q
+                codes = x_raw[j][:, BLOCK * b : BLOCK * (b + 1)].bitcast(FP8)
+                if j == S_TILE:
+                    nc.scalar.activation(out=wide[:, BLOCK * q : BLOCK * (q + 1)], in_=codes, func=ACT.Copy, scale=x_scale[:, j, b : b + 1])
+                else:
+                    nc.vector.tensor_scalar(
+                        out=sorted_view[:, 32 * q : 32 * q + 32, :, :],
+                        in0=codes.rearrange("p (r u e) -> p r u e", u=2, e=2),
+                        scalar1=x_scale[:, j, b : b + 1],
+                        scalar2=None,
+                        op0=ALU.mult,
+                    )
+            x_wide[j, g] = wide
+
+        def turn_x(j, passes):
+            bank = next_bank(("x", j, passes))
+            for i, g in enumerate(passes):
+                words = x_wide[j, g][:].bitcast(F32)
+                for u in range(2):
+                    col = (2 * i + u) * P
+                    half = words[:, u : 2 * P : 2] if j == S_TILE else words[:, u * P : (u + 1) * P]
+                    nc.tensor.transpose(bank[:, col : col + P], half, ident[:])
+            x_bank[j, passes] = bank
+
+        def copy_x(j, passes):
+            n = len(passes)
+            turned = work.tile([P, n * KPASS], BF16, name="x_turned", tag="x_turned", bufs=6, align_bytes=64)
+            mover = nc.vector.tensor_copy if j >= (V_REST if len(passes) == 1 else V_FIRST) else nc.scalar.copy
+            mover(
+                out=turned[:].bitcast(F32).rearrange("p (g m u) -> p g m u", g=n, u=2),
+                in_=x_bank[j, passes][:, : n * 2 * P].rearrange("p (g u m) -> p g m u", g=n, u=2),
+            )
+            x_turned[j, passes] = turned
+            emptied(("x", j, passes))
+
+        def quantize_x(j, passes):
+            n = len(passes)
+            codes = work.tile([P, n * P], U32, name="x_codes", tag="x_codes", bufs=12, align_bytes=64)
+            scales = work.tile([P, n * P], U8, name="x_scales", tag="x_scales", bufs=12, align_bytes=64)
+            nc.vector.quantize_mx(out=codes[:].bitcast(FP8X4), scales=scales[:], in_=x_turned[j, passes][:])
+            for i, g in enumerate(passes):
+                x_codes[j, g] = codes[:, i * P : (i + 1) * P]
+                x_scales[j, g] = scales[:, i * P : (i + 1) * P]
+
+        order = [divmod(s, HALVES) for s in range(UNITS)]
+        if SWAP:
+            order[1], order[2] = order[2], order[1]
+        acc, squares, power, envelope, y, y_narrow = {}, {}, {}, {}, {}, {}
+
+        def multiply(s, part):
+            j, h = order[s]
+            bank = next_bank(("acc", s, part))
+            for g in range(PASSES):
+                nc.tensor.matmul_mx(
+                    out=bank[:],
+                    lhsT=x_codes[j, g].bitcast(FP8X4),
+                    lhsT_scale=x_scales[j, g],
+                    rhs=w_words[part, h][:, g, :].bitcast(FP4X4),
+                    rhs_scale=w_scales[part][:, g * N + h * HALF : g * N + (h + 1) * HALF],
+                    start=(g == 0),
+                    stop=(g == PASSES - 1),
+                )
+            acc[s, part] = bank
+
+        WHOLE = slice(0, HALF)
+
+        def square(s, part, c=WHOLE):
+            if c.start == 0:
+                squares[s, part] = work.tile([P, HALF], F32, name="square", tag="square", bufs=6)
+            nc.scalar.activation(out=squares[s, part][:, c], in_=acc[s, part][:, c], func=ACT.Square)
+            if c.stop == HALF:
+                emptied(("acc", s, part))
+
+        def add(s, c=WHOLE):
+            if c.start == 0:
+                power[s] = work.tile([P, HALF], F32, name="power", tag="power", bufs=3)
+            nc.vector.tensor_tensor(out=power[s][:, c], in0=squares[s, 0][:, c], in1=squares[s, 1][:, c], op=ALU.add)
+
+        def root(s, c=WHOLE):
+            if c.start == 0:
+                envelope[s] = work.tile([P, HALF], F32, name="envelope", tag="envelope", bufs=3)
+            nc.scalar.activation(out=envelope[s][:, c], in_=power[s][:, c], func=ACT.Sqrt)
+
+        def subtract(s, c=WHOLE):
+            j, h = order[s]
+            if c.start == 0:
+                y[s] = work.tile([P, HALF], F32, name="y", tag="y", bufs=6)
+            cols = slice(h * HALF + c.start, h * HALF + c.stop)
+            nc.vector.tensor_tensor(out=y[s][:, c], in0=envelope[s][:, c], in1=thr_rows[:, cols], op=ALU.subtract)
+            if c.stop == HALF:
+                nc.sync.dma_start(out=out_0[j * P : (j + 1) * P, h * HALF : (h + 1) * HALF], in_=y[s][:])
+
+        def narrow(s, c=WHOLE):
+            if c.start == 0:
+                y_narrow[s] = work.tile([P, HALF], BF16, name="y_narrow", tag="y_narrow", bufs=6)
+            nc.vector.tensor_copy(
+                out=y_narrow[s][:].rearrange("p (u r e) -> p u r e", u=2, e=2)[:, :, c.start // 4 : c.stop // 4, :],
+                in_=y[s][:, c].rearrange("p (r u e) -> p u r e", u=2, e=2),
+            )
+
+        y_bank, y_turned, y_codes = {}, {}, {}
+        scale_spans = ((0, EARLY_SCALE_TILES), (EARLY_SCALE_TILES, TILES))
+        y_scales = {}
+        for first, last in scale_spans:
+            y_scales[first, last] = keep.tile([P, HALVES, (last - first) * P], U8, name="y_scales%d" % first, align_bytes=64)
+
+        def turn_y(units):
+            bank = next_bank(("y", units))
+            for i, s in enumerate(units):
+                words = y_narrow[s][:].bitcast(F32)
+                for u in range(2):
+                    col = (2 * i + u) * P
+                    nc.tensor.transpose(bank[:, col : col + P], words[:, u * P : (u + 1) * P], ident[:])
+            y_bank[units] = bank
+
+        def copy_y(units):
+            n = len(units)
+            turned = work.tile([P, n * HALF], BF16, name="y_turned", tag="y_turned", bufs=3, align_bytes=64)
+            mover = nc.vector.tensor_copy if V_Y <= units[0] < V_Y_END else nc.scalar.copy
+            mover(
+                out=turned[:].bitcast(F32).rearrange("p (g m u) -> p g m u", g=n, u=2),
+                in_=y_bank[units][:, : n * 2 * P].rearrange("p (g u m) -> p g m u", g=n, u=2),
+            )
+            emptied(("y", units))
+            for i, s in enumerate(units):
+                y_turned[s] = turned[:, i * HALF : (i + 1) * HALF]
+
+        def store_scales(first, last):
+            for q in range(4):
+                nc.sync.dma_start(
+                    out=out_2[:, 4 * q : 4 * q + 4, first * P : last * P].bitcast(I32).rearrange("g r m -> r g m"),
+                    in_=y_scales[first, last][32 * q : 32 * q + 4, :, :].bitcast(I32),
+                )
+
+        def quantize_y(s):
+            j, h = order[s]
+            first, last = scale_spans[j >= EARLY_SCALE_TILES]
+            if j % 2 == 0:
+                y_codes[h] = work.tile([P, 2 * P], U32, name="y_codes", tag="y_codes", bufs=6, align_bytes=64)
+            col = (j % 2) * P
+            nc.vector.quantize_mx(
+                out=y_codes[h][:, col : col + P].bitcast(FP8X4),
+                scales=y_scales[first, last][:, h, (j - first) * P : (j - first + 1) * P],
+                in_=y_turned[s],
+            )
+            if j % 2 == 1:
+                nc.sync.dma_start(
+                    out=out_1[h].rearrange("p m t -> p (m t)")[:, (j - 1) * 4 * P : (j + 1) * 4 * P].bitcast(I32),
+                    in_=y_codes[h][:].bitcast(I32),
+                )
+            if h == HALVES - 1 and j == last - 1:
+                store_scales(first, last)
+
+        def quantize_group(units):
+            for s in units:
+                quantize_y(s)
+
+        def live(s):
+            return 0 <= s < UNITS
+
+        FIRST, REST = (0, 1), (2,)
+        LAST = UNITS - 1
+
+        for g in range(PASSES):
+            widen(0, g)
+            turn_x(0, (g,))
+            copy_x(0, (g,))
+        widen(1, 0)
+        quantize_x(0, (0,))
+        widen(1, 1)
+        quantize_x(0, (1,))
+        quantize_x(0, (2,))
+        widen(1, 2)
+        for passes in (FIRST, REST):
+            turn_x(1, passes)
+            copy_x(1, passes)
+        to_widen = [(j, g) for j in range(2, TILES) for g in range(PASSES)]
+        for j, g in to_widen[:PASSES]:
+            widen(j, g)
+        for passes in (FIRST, REST):
+            quantize_x(1, passes)
+        for j, g in to_widen[PASSES : (HEAD_WIDE - 2) * PASSES]:
+            widen(j, g)
+        to_widen = to_widen[(HEAD_WIDE - 2) * PASSES :]
+        to_turn = list(range(2, TILES))
+
+        to_copy = []
+        next_y = 0
+        for s in range(UNITS):
+            if live(s):
+                multiply(s, 0)
+                multiply(s, 1)
+            copied, to_copy = to_copy[:COPIES], to_copy[COPIES:]
+            for stage, after, args in copied:
+                stage(*args)
+            if live(s):
+                square(s, 0)
+            if live(s - 2):
+                subtract(s - 2)
+            if live(s - 1):
+                add(s - 1)
+            if live(s - 1) and (s < LAST or ROOT_FIRST):
+                root(s - 1)
+            if s < LAST:
+                square(s, 1)
+            if live(s - 2):
+                narrow(s - 2)
+            for stage, after, args in copied:
+                after(*args)
+            count = WIDENS[s % 2]
+            for j, g in to_widen[:count]:
+                widen(j, g)
+            to_widen = to_widen[count:]
+            if s % 2 == 1:
+                count = 2 if s // 2 < DOUBLE_RUNS else 1
+                for j in to_turn[:count]:
+                    for passes in (FIRST, REST):
+                        turn_x(j, passes)
+                        to_copy.append((copy_x, quantize_x, (j, passes)))
+                to_turn = to_turn[count:]
+                group = tuple(range(next_y, s - Y_LAG + 2))[:2]
+                if group:
+                    turn_y(group)
+                    to_copy.append((copy_y, quantize_group, (group,)))
+                    next_y = group[-1] + 1
+        width = HALF // PIECES
+        pieces = [slice(c, c + width) for c in range(0, HALF, width)]
+        while next_y < LAST - 1:
+            group = tuple(range(next_y, LAST - 1))[:2]
+            turn_y(group)
+            to_copy.append((copy_y, quantize_group, (group,)))
+            next_y = group[-1] + 1
+        for c in pieces:
+            square(LAST, 1, c)
+        if not ROOT_FIRST:
+            root(LAST - 1)
+        if ROOT_FIRST:
+            subtract(LAST - 1)
+        for c in pieces:
+            add(LAST, c)
+            root(LAST, c)
+        if not ROOT_FIRST:
+            subtract(LAST - 1)
+        narrow(LAST - 1)
+        turn_y((LAST - 1,))
+        to_copy.append((copy_y, quantize_group, ((LAST - 1,),)))
+        for stage, after, args in to_copy:
+            stage(*args)
+        for c in pieces:
+            subtract(LAST, c)
+        for c in pieces:
+            narrow(LAST, c)
+        turn_y((LAST,))
+        copy_y((LAST,))
+        for stage, after, args in to_copy:
+            after(*args)
+        quantize_y(LAST)

@@ -27,23 +27,33 @@ UNITS = TILES * HALVES
 BLOCK = 128
 BLOCKS = K // BLOCK
 BANKS = 8
-X_LOADS = ((0, 1), (1, 3), (3, 5), (5, 10))
-EARLY_SCALE_TILES = 8
-Y_LAG = 3
+X_LOADS = ((0, 1), (1, 3), (3, 5), (5, 7), (7, 10))
 DOUBLE_RUNS = 0
-SWAP = 1
-COPIES = 2
+HEAD_TURN = 2
+I_FIRST = 0
+V_EARLY = 0
+X3_POS = 0
+V_Y = 99
+V_Y_END = 14
+EARLY_SCALE_TILES = 7
+SCALE_PITCH = 16
+EARLY_X_SCALES = 5
+WHOLE_FROM = 2
+SPLIT = 8
+MM_BANKS = 4
+Y_EVEN = 1
 WIDENS = (2, 2)
-V_REST = 99
-V_FIRST = 7
-V_Y_END = 16
-S_TILE = 99
-ROOT_FIRST = 0
-TURN1_LATE = 0
 HEAD_WIDE = 3
 PIECES = 2
-V_Y = 99
-X_POS = 0
+V_FIRST = 8
+V_REST = 99
+WARM1 = 10
+WARM2 = 8
+S_TILES = ()
+V_HEAD = 1
+Y_LAG = 1
+TURN1 = 1
+V_THR = 0
 
 
 def tile_radar_iq_envelope_planes_b2_kernel(
@@ -56,17 +66,18 @@ def tile_radar_iq_envelope_planes_b2_kernel(
         psum = ctx.enter_context(tc.psum_pool(name="psum", bufs=1))
         ctx.enter_context(tc.manual_schedule())
 
-        free_banks = list(range(BANKS))
+        free_banks = {"acc": list(range(MM_BANKS)), "turn": list(range(MM_BANKS, BANKS))}
         bank_number = {}
 
-        def next_bank(key):
-            n = free_banks[0]
-            free_banks.remove(n)
-            bank_number[key] = n
+        def next_bank(role, key):
+            n = free_banks[role][0]
+            free_banks[role].remove(n)
+            bank_number[key] = (role, n)
             return psum.tile([P, HALF], F32, name="bank%d" % n, tag="bank%d" % n)
 
         def emptied(key):
-            free_banks.append(bank_number[key])
+            role, n = bank_number[key]
+            free_banks[role].append(n)
 
         ident = keep.tile([P, P], F32, name="ident")
         make_identity(nc, ident[:])
@@ -74,10 +85,33 @@ def tile_radar_iq_envelope_planes_b2_kernel(
         w_scales = []
         for name in ("wi_scales", "wq_scales"):
             plane = keep.tile([P, PASSES * N], U8, name=name, align_bytes=64)
-            nc.vector.memset(plane[:].bitcast(I32), 0)
             w_scales.append(plane)
+        idle_values = keep.tile([P, KPASS], BF16, name="idle_values", align_bytes=64)
+        idle_codes = keep.tile([P, P], U32, name="idle_codes", align_bytes=64)
+        idle_scales = keep.tile([P, P], U8, name="idle_scales", align_bytes=64)
+        nc.vector.memset(idle_values[:].bitcast(I32), 0)
+        nc.vector.memset(w_scales[0][:].bitcast(I32), 0)
+        nc.vector.quantize_mx(out=idle_codes[:].bitcast(FP8X4), scales=idle_scales[:], in_=idle_values[:])
         nc.vector.memset(warm[:, 0:1], 1.0)
+        nc.vector.memset(w_scales[1][:].bitcast(I32), 0)
         nc.scalar.activation(out=warm[:, 1:2], in_=warm[:, 0:1], func=ACT.Sqrt)
+
+        def warm_up(count):
+            if count == 0:
+                return
+            bank = next_bank("acc", "idle")
+            for i in range(count):
+                col = (i % 4) * P
+                nc.tensor.matmul_mx(
+                    out=bank[:, col : col + P],
+                    lhsT=idle_codes[:].bitcast(FP8X4),
+                    lhsT_scale=idle_scales[:],
+                    rhs=idle_codes[:, : P // 2].bitcast(FP4X4),
+                    rhs_scale=idle_scales[:],
+                    start=True,
+                    stop=True,
+                )
+            emptied("idle")
 
         x_raw = {}
 
@@ -89,10 +123,10 @@ def tile_radar_iq_envelope_planes_b2_kernel(
 
         def load_w_scales(part):
             src = (Wi_scales, Wq_scales)[part]
-            for q in range(4):
+            for r in range(4):
                 nc.sync.dma_start(
-                    out=w_scales[part][32 * q : 32 * q + 4, :].bitcast(I32).rearrange("r (g n) -> r g n", g=PASSES),
-                    in_=src[:, 4 * q : 4 * q + 4, :].bitcast(I32).rearrange("g r n -> r g n"),
+                    out=w_scales[part][r:P:32, :].bitcast(I32).rearrange("q (g n) -> q g n", g=PASSES),
+                    in_=src[:, r:16:4, :].bitcast(I32).rearrange("g q n -> q g n"),
                 )
 
         w_words = {}
@@ -103,23 +137,50 @@ def tile_radar_iq_envelope_planes_b2_kernel(
             nc.sync.dma_start(out=words[:], in_=src[:, :, 2 * HALF * h : 2 * HALF * (h + 1)].rearrange("g p b -> p g b"))
             w_words[part, h] = words
 
+        x_scale = {}
+
+        def load_x_scales(first, last):
+            rows = keep.tile([P, last - first, SCALE_PITCH], F32, name="x_scale%d" % first)
+            nc.sync.dma_start(
+                out=rows[:, :, :BLOCKS], in_=X_scale[first * P : last * P, :].rearrange("(j p) c -> p j c", p=P)
+            )
+            for j in range(first, last):
+                x_scale[j] = rows[:, j - first, :]
+
         load_x(*X_LOADS[0])
-        x_scale = keep.tile([P, TILES, BLOCKS], F32, name="x_scale")
-        nc.sync.dma_start(out=x_scale[:], in_=X_scale.rearrange("(j p) c -> p j c", p=P))
+        load_x_scales(0, EARLY_X_SCALES)
         load_x(*X_LOADS[1])
         load_w_scales(0)
         load_w_words(0, 0)
+        thr_words = keep.tile([P, N // P], BF16, name="thr_words")
+        nc.sync.dma_start(out=thr_words[:], in_=thr.rearrange("o (p c) -> p (o c)", p=P))
         load_w_scales(1)
         load_w_words(1, 0)
-        if X_POS == 0:
+        if X3_POS == 0:
             load_x(*X_LOADS[2])
         load_w_words(0, 1)
-        load_w_words(1, 1)
-        if X_POS == 1:
+        if X3_POS == 1:
             load_x(*X_LOADS[2])
-        thr_rows = keep.tile([P, N], BF16, name="thr_rows")
-        nc.sync.dma_start(out=thr_rows[:], in_=thr.rearrange("o n -> (o n)").partition_broadcast(P))
+        load_w_words(1, 1)
+        if X3_POS == 2:
+            load_x(*X_LOADS[2])
+        load_x_scales(EARLY_X_SCALES, TILES)
         load_x(*X_LOADS[3])
+        load_x(*X_LOADS[4])
+
+        thr_rows = keep.tile([P, N], BF16, name="thr_rows")
+
+        def spread_thr():
+            bank = next_bank("turn", "thr")
+            words = thr_words[:].bitcast(F32)
+            for c in range(4):
+                nc.tensor.transpose(bank[:, c * P : (c + 1) * P], words[:, c : c + 1].to_broadcast([P, P]), ident[:])
+            mover = nc.vector.tensor_copy if V_THR else nc.scalar.copy
+            mover(
+                out=thr_rows[:].bitcast(F32).rearrange("p (j c) -> p j c", c=4),
+                in_=bank[:].rearrange("p (c j) -> p j c", c=4),
+            )
+            emptied("thr")
 
         x_wide, x_bank, x_turned, x_codes, x_scales = {}, {}, {}, {}, {}
 
@@ -129,32 +190,32 @@ def tile_radar_iq_envelope_planes_b2_kernel(
             for q in range(4):
                 b = 4 * g + q
                 codes = x_raw[j][:, BLOCK * b : BLOCK * (b + 1)].bitcast(FP8)
-                if j == S_TILE:
-                    nc.scalar.activation(out=wide[:, BLOCK * q : BLOCK * (q + 1)], in_=codes, func=ACT.Copy, scale=x_scale[:, j, b : b + 1])
+                if j in S_TILES:
+                    nc.scalar.activation(out=wide[:, BLOCK * q : BLOCK * (q + 1)], in_=codes, func=ACT.Copy, scale=x_scale[j][:, b : b + 1])
                 else:
                     nc.vector.tensor_scalar(
                         out=sorted_view[:, 32 * q : 32 * q + 32, :, :],
                         in0=codes.rearrange("p (r u e) -> p r u e", u=2, e=2),
-                        scalar1=x_scale[:, j, b : b + 1],
+                        scalar1=x_scale[j][:, b : b + 1],
                         scalar2=None,
                         op0=ALU.mult,
                     )
             x_wide[j, g] = wide
 
         def turn_x(j, passes):
-            bank = next_bank(("x", j, passes))
+            bank = next_bank("turn", ("x", j, passes))
             for i, g in enumerate(passes):
                 words = x_wide[j, g][:].bitcast(F32)
                 for u in range(2):
                     col = (2 * i + u) * P
-                    half = words[:, u : 2 * P : 2] if j == S_TILE else words[:, u * P : (u + 1) * P]
+                    half = words[:, u : 2 * P : 2] if j in S_TILES else words[:, u * P : (u + 1) * P]
                     nc.tensor.transpose(bank[:, col : col + P], half, ident[:])
             x_bank[j, passes] = bank
 
         def copy_x(j, passes):
             n = len(passes)
             turned = work.tile([P, n * KPASS], BF16, name="x_turned", tag="x_turned", bufs=6, align_bytes=64)
-            mover = nc.vector.tensor_copy if j >= (V_REST if len(passes) == 1 else V_FIRST) else nc.scalar.copy
+            mover = nc.vector.tensor_copy if (j >= (V_REST if len(passes) == 1 else V_FIRST) or (1 <= j <= V_EARLY and len(passes) == 2)) else nc.scalar.copy
             mover(
                 out=turned[:].bitcast(F32).rearrange("p (g m u) -> p g m u", g=n, u=2),
                 in_=x_bank[j, passes][:, : n * 2 * P].rearrange("p (g u m) -> p g m u", g=n, u=2),
@@ -164,21 +225,18 @@ def tile_radar_iq_envelope_planes_b2_kernel(
 
         def quantize_x(j, passes):
             n = len(passes)
-            codes = work.tile([P, n * P], U32, name="x_codes", tag="x_codes", bufs=12, align_bytes=64)
-            scales = work.tile([P, n * P], U8, name="x_scales", tag="x_scales", bufs=12, align_bytes=64)
+            codes = work.tile([P, n * P], U32, name="x_codes", tag="x_codes", bufs=16, align_bytes=64)
+            scales = work.tile([P, n * P], U8, name="x_scales", tag="x_scales", bufs=16, align_bytes=64)
             nc.vector.quantize_mx(out=codes[:].bitcast(FP8X4), scales=scales[:], in_=x_turned[j, passes][:])
             for i, g in enumerate(passes):
                 x_codes[j, g] = codes[:, i * P : (i + 1) * P]
                 x_scales[j, g] = scales[:, i * P : (i + 1) * P]
 
-        order = [divmod(s, HALVES) for s in range(UNITS)]
-        if SWAP:
-            order[1], order[2] = order[2], order[1]
         acc, squares, power, envelope, y, y_narrow = {}, {}, {}, {}, {}, {}
 
         def multiply(s, part):
-            j, h = order[s]
-            bank = next_bank(("acc", s, part))
+            j, h = divmod(s, HALVES)
+            bank = next_bank("acc", ("acc", s, part))
             for g in range(PASSES):
                 nc.tensor.matmul_mx(
                     out=bank[:],
@@ -191,41 +249,48 @@ def tile_radar_iq_envelope_planes_b2_kernel(
                 )
             acc[s, part] = bank
 
-        WHOLE = slice(0, HALF)
-
-        def square(s, part, c=WHOLE):
+        def square(j, part, c):
             if c.start == 0:
-                squares[s, part] = work.tile([P, HALF], F32, name="square", tag="square", bufs=6)
-            nc.scalar.activation(out=squares[s, part][:, c], in_=acc[s, part][:, c], func=ACT.Square)
-            if c.stop == HALF:
+                squares[j, part] = work.tile([P, N], F32, name="square", tag="square", bufs=5)
+            h = c.start // HALF
+            s = HALVES * j + h
+            nc.scalar.activation(out=squares[j, part][:, c], in_=acc[s, part][:, c.start - h * HALF : c.stop - h * HALF], func=ACT.Square)
+            if c.stop % HALF == 0:
                 emptied(("acc", s, part))
 
-        def add(s, c=WHOLE):
+        def add(j, c):
             if c.start == 0:
-                power[s] = work.tile([P, HALF], F32, name="power", tag="power", bufs=3)
-            nc.vector.tensor_tensor(out=power[s][:, c], in0=squares[s, 0][:, c], in1=squares[s, 1][:, c], op=ALU.add)
+                power[j] = work.tile([P, N], F32, name="power", tag="power", bufs=3)
+            nc.vector.tensor_tensor(out=power[j][:, c], in0=squares[j, 0][:, c], in1=squares[j, 1][:, c], op=ALU.add)
 
-        def root(s, c=WHOLE):
+        def root(j, c):
             if c.start == 0:
-                envelope[s] = work.tile([P, HALF], F32, name="envelope", tag="envelope", bufs=3)
-            nc.scalar.activation(out=envelope[s][:, c], in_=power[s][:, c], func=ACT.Sqrt)
+                envelope[j] = work.tile([P, N], F32, name="envelope", tag="envelope", bufs=3)
+            nc.scalar.activation(out=envelope[j][:, c], in_=power[j][:, c], func=ACT.Sqrt)
 
-        def subtract(s, c=WHOLE):
-            j, h = order[s]
+        def subtract(j, c):
             if c.start == 0:
-                y[s] = work.tile([P, HALF], F32, name="y", tag="y", bufs=6)
-            cols = slice(h * HALF + c.start, h * HALF + c.stop)
-            nc.vector.tensor_tensor(out=y[s][:, c], in0=envelope[s][:, c], in1=thr_rows[:, cols], op=ALU.subtract)
-            if c.stop == HALF:
-                nc.sync.dma_start(out=out_0[j * P : (j + 1) * P, h * HALF : (h + 1) * HALF], in_=y[s][:])
+                y[j] = work.tile([P, N], F32, name="y", tag="y", bufs=4)
+            nc.vector.tensor_tensor(out=y[j][:, c], in0=envelope[j][:, c], in1=thr_rows[:, c], op=ALU.subtract)
+            if c.stop % HALF == 0:
+                stored = c if c.stop - c.start >= HALF else slice(c.stop - HALF, c.stop)
+                nc.sync.dma_start(out=out_0[j * P : (j + 1) * P, stored], in_=y[j][:, stored])
 
-        def narrow(s, c=WHOLE):
+        def narrow(j, c):
             if c.start == 0:
-                y_narrow[s] = work.tile([P, HALF], BF16, name="y_narrow", tag="y_narrow", bufs=6)
-            nc.vector.tensor_copy(
-                out=y_narrow[s][:].rearrange("p (u r e) -> p u r e", u=2, e=2)[:, :, c.start // 4 : c.stop // 4, :],
-                in_=y[s][:, c].rearrange("p (r u e) -> p u r e", u=2, e=2),
-            )
+                y_narrow[j] = work.tile([P, N], BF16, name="y_narrow", tag="y_narrow", bufs=4)
+            if c.stop - c.start == N:
+                nc.vector.tensor_copy(
+                    out=y_narrow[j][:].rearrange("p (h u r e) -> p h u r e", h=HALVES, u=2, e=2),
+                    in_=y[j][:].rearrange("p (h r u e) -> p h u r e", h=HALVES, u=2, e=2),
+                )
+            else:
+                h = c.start // HALF
+                rows = slice((c.start - h * HALF) // 4, (c.stop - h * HALF) // 4)
+                nc.vector.tensor_copy(
+                    out=y_narrow[j][:].rearrange("p (h u r e) -> p h u r e", h=HALVES, u=2, e=2)[:, h, :, rows, :],
+                    in_=y[j][:, c].rearrange("p (r u e) -> p u r e", u=2, e=2),
+                )
 
         y_bank, y_turned, y_codes = {}, {}, {}
         scale_spans = ((0, EARLY_SCALE_TILES), (EARLY_SCALE_TILES, TILES))
@@ -234,9 +299,9 @@ def tile_radar_iq_envelope_planes_b2_kernel(
             y_scales[first, last] = keep.tile([P, HALVES, (last - first) * P], U8, name="y_scales%d" % first, align_bytes=64)
 
         def turn_y(units):
-            bank = next_bank(("y", units))
+            bank = next_bank("turn", ("y", units))
             for i, s in enumerate(units):
-                words = y_narrow[s][:].bitcast(F32)
+                words = y_narrow[s // HALVES][:, (s % HALVES) * HALF : (s % HALVES + 1) * HALF].bitcast(F32)
                 for u in range(2):
                     col = (2 * i + u) * P
                     nc.tensor.transpose(bank[:, col : col + P], words[:, u * P : (u + 1) * P], ident[:])
@@ -244,7 +309,7 @@ def tile_radar_iq_envelope_planes_b2_kernel(
 
         def copy_y(units):
             n = len(units)
-            turned = work.tile([P, n * HALF], BF16, name="y_turned", tag="y_turned", bufs=3, align_bytes=64)
+            turned = work.tile([P, n * HALF], BF16, name="y_turned", tag="y_turned", bufs=5, align_bytes=64)
             mover = nc.vector.tensor_copy if V_Y <= units[0] < V_Y_END else nc.scalar.copy
             mover(
                 out=turned[:].bitcast(F32).rearrange("p (g m u) -> p g m u", g=n, u=2),
@@ -255,14 +320,14 @@ def tile_radar_iq_envelope_planes_b2_kernel(
                 y_turned[s] = turned[:, i * HALF : (i + 1) * HALF]
 
         def store_scales(first, last):
-            for q in range(4):
+            for q in (0, 2, 1, 3):
                 nc.sync.dma_start(
                     out=out_2[:, 4 * q : 4 * q + 4, first * P : last * P].bitcast(I32).rearrange("g r m -> r g m"),
                     in_=y_scales[first, last][32 * q : 32 * q + 4, :, :].bitcast(I32),
                 )
 
         def quantize_y(s):
-            j, h = order[s]
+            j, h = divmod(s, HALVES)
             first, last = scale_spans[j >= EARLY_SCALE_TILES]
             if j % 2 == 0:
                 y_codes[h] = work.tile([P, 2 * P], U32, name="y_codes", tag="y_codes", bufs=6, align_bytes=64)
@@ -284,103 +349,146 @@ def tile_radar_iq_envelope_planes_b2_kernel(
             for s in units:
                 quantize_y(s)
 
-        def live(s):
-            return 0 <= s < UNITS
-
         FIRST, REST = (0, 1), (2,)
         LAST = UNITS - 1
+        ALL = slice(0, N)
 
+        def half(u):
+            return u // HALVES, slice((u % HALVES) * HALF, (u % HALVES + 1) * HALF)
+
+        order = [0, 2, 1, 3] + list(range(4, UNITS))
+        halves_done, wholes_done = {}, {}
+        for s, u in enumerate(order):
+            if WHOLE_FROM <= u // HALVES < SPLIT:
+                if u % HALVES == 1:
+                    wholes_done[s] = u // HALVES
+            else:
+                halves_done[s] = u
+
+        warm_up(WARM1)
         for g in range(PASSES):
             widen(0, g)
             turn_x(0, (g,))
             copy_x(0, (g,))
-        widen(1, 0)
-        quantize_x(0, (0,))
-        widen(1, 1)
-        quantize_x(0, (1,))
-        quantize_x(0, (2,))
-        widen(1, 2)
+        warm_up(WARM2)
+        for g in range(PASSES):
+            widen(1, g)
+            quantize_x(0, (g,))
+        for g in range(PASSES):
+            widen(2, g)
         for passes in (FIRST, REST):
             turn_x(1, passes)
             copy_x(1, passes)
-        to_widen = [(j, g) for j in range(2, TILES) for g in range(PASSES)]
-        for j, g in to_widen[:PASSES]:
-            widen(j, g)
+        multiply(0, 0)
+        square(0, 0, half(0)[1])
         for passes in (FIRST, REST):
             quantize_x(1, passes)
-        for j, g in to_widen[PASSES : (HEAD_WIDE - 2) * PASSES]:
-            widen(j, g)
-        to_widen = to_widen[(HEAD_WIDE - 2) * PASSES :]
-        to_turn = list(range(2, TILES))
-
+        to_turn = list(range(HEAD_TURN, TILES))
         to_copy = []
-        next_y = 0
-        for s in range(UNITS):
-            if live(s):
-                multiply(s, 0)
-                multiply(s, 1)
-            copied, to_copy = to_copy[:COPIES], to_copy[COPIES:]
-            for stage, after, args in copied:
-                stage(*args)
-            if live(s):
-                square(s, 0)
-            if live(s - 2):
-                subtract(s - 2)
-            if live(s - 1):
-                add(s - 1)
-            if live(s - 1) and (s < LAST or ROOT_FIRST):
-                root(s - 1)
+        if HEAD_TURN == 3:
+            for passes in (FIRST, REST):
+                turn_x(2, passes)
+            to_copy.append(2)
+        spread_thr()
+        if I_FIRST:
+            multiply(order[1], 0)
+        multiply(0, 1)
+        to_widen = [(j, g) for j in range(3, TILES) for g in range(PASSES)]
+        late_head = to_widen[: (HEAD_WIDE - 3) * PASSES]
+        to_widen = to_widen[(HEAD_WIDE - 3) * PASSES :]
+
+        narrowed, y_groups = [], []
+        for s, u in enumerate(order):
+            step_tile, h = divmod(s, HALVES)
+            j, cols = half(u)
+            if s > I_FIRST:
+                multiply(u, 0)
+            if s > 0:
+                multiply(u, 1)
+            turned = to_copy[:1]
+            to_copy = to_copy[1:]
+            for tile in turned:
+                copy_x(tile, FIRST)
+                copy_x(tile, REST)
+            copied = ()
+            if y_groups and h != Y_EVEN:
+                copied = y_groups[0]
+                y_groups = y_groups[1:]
+                copy_y(copied)
+            if s > 0:
+                square(j, 0, cols)
+            if s == 0:
+                for tile, g in late_head:
+                    widen(tile, g)
+            if s - 2 in halves_done:
+                subtract(*half(halves_done[s - 2]))
+            if s - 1 in wholes_done:
+                add(wholes_done[s - 1], ALL)
+                root(wholes_done[s - 1], ALL)
+            if s - 1 in halves_done:
+                add(*half(halves_done[s - 1]))
+                if s < LAST:
+                    root(*half(halves_done[s - 1]))
             if s < LAST:
-                square(s, 1)
-            if live(s - 2):
-                narrow(s - 2)
-            for stage, after, args in copied:
-                after(*args)
-            count = WIDENS[s % 2]
-            for j, g in to_widen[:count]:
-                widen(j, g)
+                square(j, 1, cols)
+            if s - 3 in wholes_done:
+                tile = wholes_done[s - 3]
+                narrow(tile, ALL)
+                narrowed.extend([(s, HALVES * tile), (s, HALVES * tile + 1)])
+            if s - 2 in halves_done:
+                narrow(*half(halves_done[s - 2]))
+                narrowed.append((s, halves_done[s - 2]))
+            for tile in turned:
+                quantize_x(tile, FIRST)
+                quantize_x(tile, REST)
+            count = WIDENS[h]
+            for tile, g in to_widen[:count]:
+                widen(tile, g)
             to_widen = to_widen[count:]
-            if s % 2 == 1:
-                count = 2 if s // 2 < DOUBLE_RUNS else 1
-                for j in to_turn[:count]:
-                    for passes in (FIRST, REST):
-                        turn_x(j, passes)
-                        to_copy.append((copy_x, quantize_x, (j, passes)))
+            quantize_group(copied)
+            if s - 2 in wholes_done:
+                subtract(wholes_done[s - 2], ALL)
+            if h == 1:
+                count = 2 if step_tile < DOUBLE_RUNS else 1
+                for tile in to_turn[:count]:
+                    turn_x(tile, FIRST)
+                    turn_x(tile, REST)
+                    to_copy.append(tile)
                 to_turn = to_turn[count:]
-                group = tuple(range(next_y, s - Y_LAG + 2))[:2]
-                if group:
+                group = tuple(unit for when, unit in narrowed if when <= s - Y_LAG)[:2]
+                if group and s < LAST:
                     turn_y(group)
-                    to_copy.append((copy_y, quantize_group, (group,)))
-                    next_y = group[-1] + 1
+                    y_groups.append(group)
+                    narrowed = narrowed[len(group) :]
+
         width = HALF // PIECES
-        pieces = [slice(c, c + width) for c in range(0, HALF, width)]
-        while next_y < LAST - 1:
-            group = tuple(range(next_y, LAST - 1))[:2]
+        pieces = [slice(c, c + width) for c in range(HALF, N, width)]
+        j = TILES - 1
+        waiting = [u for when, u in narrowed]
+        for i in range(0, len(waiting), 2):
+            group = tuple(waiting[i : i + 2])
             turn_y(group)
-            to_copy.append((copy_y, quantize_group, (group,)))
-            next_y = group[-1] + 1
+            y_groups.append(group)
         for c in pieces:
-            square(LAST, 1, c)
-        if not ROOT_FIRST:
-            root(LAST - 1)
-        if ROOT_FIRST:
-            subtract(LAST - 1)
+            square(j, 1, c)
+        root(*half(LAST - 1))
         for c in pieces:
-            add(LAST, c)
-            root(LAST, c)
-        if not ROOT_FIRST:
-            subtract(LAST - 1)
-        narrow(LAST - 1)
+            add(j, c)
+            root(j, c)
+        subtract(*half(LAST - 1))
+        for group in y_groups:
+            copy_y(group)
+        subtract(j, pieces[0])
+        narrow(*half(LAST - 1))
         turn_y((LAST - 1,))
-        to_copy.append((copy_y, quantize_group, ((LAST - 1,),)))
-        for stage, after, args in to_copy:
-            stage(*args)
+        copy_y((LAST - 1,))
+        for c in pieces[1:]:
+            subtract(j, c)
         for c in pieces:
-            subtract(LAST, c)
-        for c in pieces:
-            narrow(LAST, c)
+            narrow(j, c)
         turn_y((LAST,))
         copy_y((LAST,))
-        for stage, after, args in to_copy:
-            after(*args)
+        for group in y_groups:
+            quantize_group(group)
+        quantize_y(LAST - 1)
         quantize_y(LAST)

@@ -18,42 +18,26 @@ ALU = mybir.AluOpType
 ACT = mybir.ActivationFunctionType
 
 P = 128
-KPASS = 512
-PASSES = K // KPASS
-HALF = 512
-HALVES = N // HALF
+PASS = 512
+PASSES = K // PASS
+HALVES = N // PASS
 TILES = T // P
 UNITS = TILES * HALVES
-BLOCK = 128
-BLOCKS = K // BLOCK
+STORED_BLOCK = 128
+STORED_BLOCKS = K // STORED_BLOCK
+STORED_PITCH = 16
+QUADRANTS = 4
+
 BANKS = 8
+PRODUCT_BANKS = 4
 X_LOADS = ((0, 1), (1, 3), (3, 5), (5, 7), (7, 10))
-DOUBLE_RUNS = 0
-HEAD_TURN = 2
-I_FIRST = 0
-V_EARLY = 0
-X3_POS = 0
-V_Y = 99
-V_Y_END = 14
-EARLY_SCALE_TILES = 7
-SCALE_PITCH = 16
-EARLY_X_SCALES = 5
-WHOLE_FROM = 2
-SPLIT = 8
-MM_BANKS = 4
-Y_EVEN = 1
-WIDENS = (2, 2)
-HEAD_WIDE = 3
-PIECES = 2
-V_FIRST = 8
-V_REST = 99
-WARM1 = 10
-WARM2 = 8
-S_TILES = ()
-V_HEAD = 1
-Y_LAG = 1
-TURN1 = 1
-V_THR = 0
+EARLY_SCALE_LOAD = 5
+WHOLE_FROM, WHOLE_TO = 2, 8
+WIDEN_PER_STEP = 2
+VECTOR_COPIES_FROM = 7
+LAST_PIECES = 2
+EARLY_PLANE_TILES = 6
+WARM_UP = (14, 8)
 
 
 def tile_radar_iq_envelope_planes_b2_kernel(
@@ -66,42 +50,40 @@ def tile_radar_iq_envelope_planes_b2_kernel(
         psum = ctx.enter_context(tc.psum_pool(name="psum", bufs=1))
         ctx.enter_context(tc.manual_schedule())
 
-        free_banks = {"acc": list(range(MM_BANKS)), "turn": list(range(MM_BANKS, BANKS))}
-        bank_number = {}
+        free_banks = {"product": list(range(PRODUCT_BANKS)), "turn": list(range(PRODUCT_BANKS, BANKS))}
+        bank_of = {}
 
         def next_bank(role, key):
-            n = free_banks[role][0]
-            free_banks[role].remove(n)
-            bank_number[key] = (role, n)
-            return psum.tile([P, HALF], F32, name="bank%d" % n, tag="bank%d" % n)
+            number = free_banks[role][0]
+            free_banks[role].remove(number)
+            bank_of[key] = (role, number)
+            return psum.tile([P, PASS], F32, name="bank%d" % number, tag="bank%d" % number)
 
         def emptied(key):
-            role, n = bank_number[key]
-            free_banks[role].append(n)
+            role, number = bank_of[key]
+            free_banks[role].append(number)
 
         ident = keep.tile([P, P], F32, name="ident")
         make_identity(nc, ident[:])
-        warm = keep.tile([P, 2], F32, name="warm")
+        table_probe = keep.tile([P, 2], F32, name="table_probe")
         w_scales = []
         for name in ("wi_scales", "wq_scales"):
-            plane = keep.tile([P, PASSES * N], U8, name=name, align_bytes=64)
-            w_scales.append(plane)
-        idle_values = keep.tile([P, KPASS], BF16, name="idle_values", align_bytes=64)
+            scale_tile = keep.tile([P, PASSES * N], U8, name=name, align_bytes=64)
+            w_scales.append(scale_tile)
+        idle_values = keep.tile([P, PASS], BF16, name="idle_values", align_bytes=64)
         idle_codes = keep.tile([P, P], U32, name="idle_codes", align_bytes=64)
         idle_scales = keep.tile([P, P], U8, name="idle_scales", align_bytes=64)
         nc.vector.memset(idle_values[:].bitcast(I32), 0)
         nc.vector.memset(w_scales[0][:].bitcast(I32), 0)
         nc.vector.quantize_mx(out=idle_codes[:].bitcast(FP8X4), scales=idle_scales[:], in_=idle_values[:])
-        nc.vector.memset(warm[:, 0:1], 1.0)
+        nc.vector.memset(table_probe[:, 0:1], 1.0)
         nc.vector.memset(w_scales[1][:].bitcast(I32), 0)
-        nc.scalar.activation(out=warm[:, 1:2], in_=warm[:, 0:1], func=ACT.Sqrt)
+        nc.scalar.activation(out=table_probe[:, 1:2], in_=table_probe[:, 0:1], func=ACT.Sqrt)
 
         def warm_up(count):
-            if count == 0:
-                return
-            bank = next_bank("acc", "idle")
+            bank = next_bank("product", "idle")
             for i in range(count):
-                col = (i % 4) * P
+                col = (i % (PASS // P)) * P
                 nc.tensor.matmul_mx(
                     out=bank[:, col : col + P],
                     lhsT=idle_codes[:].bitcast(FP8X4),
@@ -113,13 +95,22 @@ def tile_radar_iq_envelope_planes_b2_kernel(
                 )
             emptied("idle")
 
-        x_raw = {}
+        x_raw, x_stored_scale, w_words = {}, {}, {}
 
         def load_x(first, last):
             raw = keep.tile([P, last - first, K], U8, name="x_raw%d" % first)
             nc.sync.dma_start(out=raw[:], in_=X_bytes[first * P : last * P, :].rearrange("(j p) k -> p j k", p=P))
             for j in range(first, last):
                 x_raw[j] = raw[:, j - first, :]
+
+        def load_x_scales(first, last):
+            rows = keep.tile([P, last - first, STORED_PITCH], F32, name="x_stored_scale%d" % first)
+            nc.sync.dma_start(
+                out=rows[:, :, :STORED_BLOCKS],
+                in_=X_scale[first * P : last * P, :].rearrange("(j p) c -> p j c", p=P),
+            )
+            for j in range(first, last):
+                x_stored_scale[j] = rows[:, j - first, :]
 
         def load_w_scales(part):
             src = (Wi_scales, Wq_scales)[part]
@@ -129,26 +120,16 @@ def tile_radar_iq_envelope_planes_b2_kernel(
                     in_=src[:, r:16:4, :].bitcast(I32).rearrange("g q n -> q g n"),
                 )
 
-        w_words = {}
-
         def load_w_words(part, h):
             src = (Wi_words, Wq_words)[part]
-            words = keep.tile([P, PASSES, 2 * HALF], U8, name="w_words%d%d" % (part, h), align_bytes=64)
-            nc.sync.dma_start(out=words[:], in_=src[:, :, 2 * HALF * h : 2 * HALF * (h + 1)].rearrange("g p b -> p g b"))
+            words = keep.tile([P, PASSES, 2 * PASS], U8, name="w_words%d%d" % (part, h), align_bytes=64)
+            nc.sync.dma_start(
+                out=words[:], in_=src[:, :, 2 * PASS * h : 2 * PASS * (h + 1)].rearrange("g p b -> p g b")
+            )
             w_words[part, h] = words
 
-        x_scale = {}
-
-        def load_x_scales(first, last):
-            rows = keep.tile([P, last - first, SCALE_PITCH], F32, name="x_scale%d" % first)
-            nc.sync.dma_start(
-                out=rows[:, :, :BLOCKS], in_=X_scale[first * P : last * P, :].rearrange("(j p) c -> p j c", p=P)
-            )
-            for j in range(first, last):
-                x_scale[j] = rows[:, j - first, :]
-
         load_x(*X_LOADS[0])
-        load_x_scales(0, EARLY_X_SCALES)
+        load_x_scales(0, EARLY_SCALE_LOAD)
         load_x(*X_LOADS[1])
         load_w_scales(0)
         load_w_words(0, 0)
@@ -156,15 +137,10 @@ def tile_radar_iq_envelope_planes_b2_kernel(
         nc.sync.dma_start(out=thr_words[:], in_=thr.rearrange("o (p c) -> p (o c)", p=P))
         load_w_scales(1)
         load_w_words(1, 0)
-        if X3_POS == 0:
-            load_x(*X_LOADS[2])
+        load_x(*X_LOADS[2])
         load_w_words(0, 1)
-        if X3_POS == 1:
-            load_x(*X_LOADS[2])
         load_w_words(1, 1)
-        if X3_POS == 2:
-            load_x(*X_LOADS[2])
-        load_x_scales(EARLY_X_SCALES, TILES)
+        load_x_scales(EARLY_SCALE_LOAD, TILES)
         load_x(*X_LOADS[3])
         load_x(*X_LOADS[4])
 
@@ -175,8 +151,7 @@ def tile_radar_iq_envelope_planes_b2_kernel(
             words = thr_words[:].bitcast(F32)
             for c in range(4):
                 nc.tensor.transpose(bank[:, c * P : (c + 1) * P], words[:, c : c + 1].to_broadcast([P, P]), ident[:])
-            mover = nc.vector.tensor_copy if V_THR else nc.scalar.copy
-            mover(
+            nc.scalar.copy(
                 out=thr_rows[:].bitcast(F32).rearrange("p (j c) -> p j c", c=4),
                 in_=bank[:].rearrange("p (c j) -> p j c", c=4),
             )
@@ -185,310 +160,294 @@ def tile_radar_iq_envelope_planes_b2_kernel(
         x_wide, x_bank, x_turned, x_codes, x_scales = {}, {}, {}, {}, {}
 
         def widen(j, g):
-            wide = work.tile([P, KPASS], BF16, name="x_wide", tag="x_wide", bufs=15)
-            sorted_view = wide[:].rearrange("p (u r e) -> p r u e", u=2, e=2)
-            for q in range(4):
-                b = 4 * g + q
-                codes = x_raw[j][:, BLOCK * b : BLOCK * (b + 1)].bitcast(FP8)
-                if j in S_TILES:
-                    nc.scalar.activation(out=wide[:, BLOCK * q : BLOCK * (q + 1)], in_=codes, func=ACT.Copy, scale=x_scale[j][:, b : b + 1])
-                else:
-                    nc.vector.tensor_scalar(
-                        out=sorted_view[:, 32 * q : 32 * q + 32, :, :],
-                        in0=codes.rearrange("p (r u e) -> p r u e", u=2, e=2),
-                        scalar1=x_scale[j][:, b : b + 1],
-                        scalar2=None,
-                        op0=ALU.mult,
-                    )
+            wide = work.tile([P, PASS], BF16, name="x_wide", tag="x_wide", bufs=15)
+            for q in range(PASS // STORED_BLOCK):
+                b = (PASS // STORED_BLOCK) * g + q
+                nc.vector.tensor_scalar(
+                    out=wide[:, STORED_BLOCK * q : STORED_BLOCK * (q + 1)],
+                    in0=x_raw[j][:, STORED_BLOCK * b : STORED_BLOCK * (b + 1)].bitcast(FP8),
+                    scalar1=x_stored_scale[j][:, b : b + 1],
+                    scalar2=None,
+                    op0=ALU.mult,
+                )
             x_wide[j, g] = wide
 
-        def turn_x(j, passes):
-            bank = next_bank("turn", ("x", j, passes))
-            for i, g in enumerate(passes):
-                words = x_wide[j, g][:].bitcast(F32)
+        def turn_x(batch):
+            bank = next_bank("turn", ("x", batch))
+            for i, key in enumerate(batch):
+                words = x_wide[key][:].bitcast(F32)
                 for u in range(2):
                     col = (2 * i + u) * P
-                    half = words[:, u : 2 * P : 2] if j in S_TILES else words[:, u * P : (u + 1) * P]
-                    nc.tensor.transpose(bank[:, col : col + P], half, ident[:])
-            x_bank[j, passes] = bank
+                    nc.tensor.transpose(bank[:, col : col + P], words[:, u : 2 * P : 2], ident[:])
+            x_bank[batch] = bank
 
-        def copy_x(j, passes):
-            n = len(passes)
-            turned = work.tile([P, n * KPASS], BF16, name="x_turned", tag="x_turned", bufs=6, align_bytes=64)
-            mover = nc.vector.tensor_copy if (j >= (V_REST if len(passes) == 1 else V_FIRST) or (1 <= j <= V_EARLY and len(passes) == 2)) else nc.scalar.copy
-            mover(
-                out=turned[:].bitcast(F32).rearrange("p (g m u) -> p g m u", g=n, u=2),
-                in_=x_bank[j, passes][:, : n * 2 * P].rearrange("p (g u m) -> p g m u", g=n, u=2),
+        def copy_x(batch):
+            count = len(batch)
+            turned = work.tile([P, count * PASS], BF16, name="x_turned", tag="x_turned", bufs=6, align_bytes=64)
+            on_vector = count == 2 and batch[0][0] >= VECTOR_COPIES_FROM
+            copy = nc.vector.tensor_copy if on_vector else nc.scalar.copy
+            copy(
+                out=turned[:].bitcast(F32).rearrange("p (g m u) -> p g m u", g=count, u=2),
+                in_=x_bank[batch][:, : count * 2 * P].rearrange("p (g u m) -> p g m u", g=count, u=2),
             )
-            x_turned[j, passes] = turned
-            emptied(("x", j, passes))
+            x_turned[batch] = turned
+            emptied(("x", batch))
 
-        def quantize_x(j, passes):
-            n = len(passes)
-            codes = work.tile([P, n * P], U32, name="x_codes", tag="x_codes", bufs=16, align_bytes=64)
-            scales = work.tile([P, n * P], U8, name="x_scales", tag="x_scales", bufs=16, align_bytes=64)
-            nc.vector.quantize_mx(out=codes[:].bitcast(FP8X4), scales=scales[:], in_=x_turned[j, passes][:])
-            for i, g in enumerate(passes):
-                x_codes[j, g] = codes[:, i * P : (i + 1) * P]
-                x_scales[j, g] = scales[:, i * P : (i + 1) * P]
+        def quantize_x(batch):
+            count = len(batch)
+            codes = work.tile([P, count * P], U32, name="x_codes", tag="x_codes", bufs=16, align_bytes=64)
+            scales = work.tile([P, count * P], U8, name="x_scales", tag="x_scales", bufs=16, align_bytes=64)
+            nc.vector.quantize_mx(out=codes[:].bitcast(FP8X4), scales=scales[:], in_=x_turned[batch][:])
+            for i, key in enumerate(batch):
+                x_codes[key] = codes[:, i * P : (i + 1) * P]
+                x_scales[key] = scales[:, i * P : (i + 1) * P]
 
-        acc, squares, power, envelope, y, y_narrow = {}, {}, {}, {}, {}, {}
+        def x_batches(j):
+            return [((j, 0), (j, 1)), ((j, 2),)]
 
-        def multiply(s, part):
-            j, h = divmod(s, HALVES)
-            bank = next_bank("acc", ("acc", s, part))
+        product, squares, power, envelope, y, y_narrow = {}, {}, {}, {}, {}, {}
+
+        def multiply(unit, part):
+            j, h = divmod(unit, HALVES)
+            bank = next_bank("product", ("product", unit, part))
             for g in range(PASSES):
                 nc.tensor.matmul_mx(
                     out=bank[:],
                     lhsT=x_codes[j, g].bitcast(FP8X4),
                     lhsT_scale=x_scales[j, g],
                     rhs=w_words[part, h][:, g, :].bitcast(FP4X4),
-                    rhs_scale=w_scales[part][:, g * N + h * HALF : g * N + (h + 1) * HALF],
+                    rhs_scale=w_scales[part][:, g * N + h * PASS : g * N + (h + 1) * PASS],
                     start=(g == 0),
                     stop=(g == PASSES - 1),
                 )
-            acc[s, part] = bank
+            product[unit, part] = bank
 
-        def square(j, part, c):
-            if c.start == 0:
+        def square(j, cols, part):
+            if cols.start == 0:
                 squares[j, part] = work.tile([P, N], F32, name="square", tag="square", bufs=5)
-            h = c.start // HALF
-            s = HALVES * j + h
-            nc.scalar.activation(out=squares[j, part][:, c], in_=acc[s, part][:, c.start - h * HALF : c.stop - h * HALF], func=ACT.Square)
-            if c.stop % HALF == 0:
-                emptied(("acc", s, part))
+            h = cols.start // PASS
+            unit = HALVES * j + h
+            nc.scalar.activation(
+                out=squares[j, part][:, cols],
+                in_=product[unit, part][:, cols.start - h * PASS : cols.stop - h * PASS],
+                func=ACT.Square,
+            )
+            if cols.stop % PASS == 0:
+                emptied(("product", unit, part))
 
-        def add(j, c):
-            if c.start == 0:
+        def add(j, cols):
+            if cols.start == 0:
                 power[j] = work.tile([P, N], F32, name="power", tag="power", bufs=3)
-            nc.vector.tensor_tensor(out=power[j][:, c], in0=squares[j, 0][:, c], in1=squares[j, 1][:, c], op=ALU.add)
+            nc.vector.tensor_tensor(
+                out=power[j][:, cols], in0=squares[j, 0][:, cols], in1=squares[j, 1][:, cols], op=ALU.add
+            )
 
-        def root(j, c):
-            if c.start == 0:
+        def root(j, cols):
+            if cols.start == 0:
                 envelope[j] = work.tile([P, N], F32, name="envelope", tag="envelope", bufs=3)
-            nc.scalar.activation(out=envelope[j][:, c], in_=power[j][:, c], func=ACT.Sqrt)
+            nc.scalar.activation(out=envelope[j][:, cols], in_=power[j][:, cols], func=ACT.Sqrt)
 
-        def subtract(j, c):
-            if c.start == 0:
+        def subtract(j, cols):
+            if cols.start == 0:
                 y[j] = work.tile([P, N], F32, name="y", tag="y", bufs=4)
-            nc.vector.tensor_tensor(out=y[j][:, c], in0=envelope[j][:, c], in1=thr_rows[:, c], op=ALU.subtract)
-            if c.stop % HALF == 0:
-                stored = c if c.stop - c.start >= HALF else slice(c.stop - HALF, c.stop)
+            nc.vector.tensor_tensor(out=y[j][:, cols], in0=envelope[j][:, cols], in1=thr_rows[:, cols], op=ALU.subtract)
+            if cols.stop % PASS == 0:
+                stored = slice(min(cols.start, cols.stop - PASS), cols.stop)
                 nc.sync.dma_start(out=out_0[j * P : (j + 1) * P, stored], in_=y[j][:, stored])
 
-        def narrow(j, c):
-            if c.start == 0:
-                y_narrow[j] = work.tile([P, N], BF16, name="y_narrow", tag="y_narrow", bufs=4)
-            if c.stop - c.start == N:
+        def narrow(j, cols):
+            if cols.start == 0:
+                y_narrow[j] = work.tile([P, N], BF16, name="y_narrow", tag="y_narrow", bufs=5)
+            sorted_view = y_narrow[j][:].rearrange("p (h u r e) -> p h u r e", h=HALVES, u=2, e=2)
+            if cols.stop - cols.start == N:
                 nc.vector.tensor_copy(
-                    out=y_narrow[j][:].rearrange("p (h u r e) -> p h u r e", h=HALVES, u=2, e=2),
-                    in_=y[j][:].rearrange("p (h r u e) -> p h u r e", h=HALVES, u=2, e=2),
+                    out=sorted_view, in_=y[j][:].rearrange("p (h r u e) -> p h u r e", h=HALVES, u=2, e=2)
                 )
             else:
-                h = c.start // HALF
-                rows = slice((c.start - h * HALF) // 4, (c.stop - h * HALF) // 4)
+                h = cols.start // PASS
+                rows = slice((cols.start - h * PASS) // 4, (cols.stop - h * PASS) // 4)
                 nc.vector.tensor_copy(
-                    out=y_narrow[j][:].rearrange("p (h u r e) -> p h u r e", h=HALVES, u=2, e=2)[:, h, :, rows, :],
-                    in_=y[j][:, c].rearrange("p (r u e) -> p u r e", u=2, e=2),
+                    out=sorted_view[:, h, :, rows, :], in_=y[j][:, cols].rearrange("p (r u e) -> p u r e", u=2, e=2)
                 )
 
-        y_bank, y_turned, y_codes = {}, {}, {}
-        scale_spans = ((0, EARLY_SCALE_TILES), (EARLY_SCALE_TILES, TILES))
-        y_scales = {}
+        y_bank, y_turned, y_codes, y_scales = {}, {}, {}, {}
+        scale_spans = ((0, EARLY_PLANE_TILES), (EARLY_PLANE_TILES, TILES))
         for first, last in scale_spans:
-            y_scales[first, last] = keep.tile([P, HALVES, (last - first) * P], U8, name="y_scales%d" % first, align_bytes=64)
+            y_scales[first, last] = keep.tile(
+                [P, HALVES, (last - first) * P], U8, name="y_scales%d" % first, align_bytes=64
+            )
 
-        def turn_y(units):
-            bank = next_bank("turn", ("y", units))
-            for i, s in enumerate(units):
-                words = y_narrow[s // HALVES][:, (s % HALVES) * HALF : (s % HALVES + 1) * HALF].bitcast(F32)
+        def turn_y(group):
+            bank = next_bank("turn", ("y", group))
+            for i, unit in enumerate(group):
+                j, h = divmod(unit, HALVES)
+                words = y_narrow[j][:, h * PASS : (h + 1) * PASS].bitcast(F32)
                 for u in range(2):
                     col = (2 * i + u) * P
                     nc.tensor.transpose(bank[:, col : col + P], words[:, u * P : (u + 1) * P], ident[:])
-            y_bank[units] = bank
+            y_bank[group] = bank
 
-        def copy_y(units):
-            n = len(units)
-            turned = work.tile([P, n * HALF], BF16, name="y_turned", tag="y_turned", bufs=5, align_bytes=64)
-            mover = nc.vector.tensor_copy if V_Y <= units[0] < V_Y_END else nc.scalar.copy
-            mover(
-                out=turned[:].bitcast(F32).rearrange("p (g m u) -> p g m u", g=n, u=2),
-                in_=y_bank[units][:, : n * 2 * P].rearrange("p (g u m) -> p g m u", g=n, u=2),
+        def copy_y(group):
+            count = len(group)
+            turned = work.tile([P, count * PASS], BF16, name="y_turned", tag="y_turned", bufs=5, align_bytes=64)
+            nc.scalar.copy(
+                out=turned[:].bitcast(F32).rearrange("p (g m u) -> p g m u", g=count, u=2),
+                in_=y_bank[group][:, : count * 2 * P].rearrange("p (g u m) -> p g m u", g=count, u=2),
             )
-            emptied(("y", units))
-            for i, s in enumerate(units):
-                y_turned[s] = turned[:, i * HALF : (i + 1) * HALF]
+            emptied(("y", group))
+            y_turned[group] = turned
 
         def store_scales(first, last):
-            for q in (0, 2, 1, 3):
-                nc.sync.dma_start(
+            for i, q in enumerate((0, 2, 1, 3)):
+                queue = nc.scalar if last == TILES and i < QUADRANTS // 2 else nc.sync
+                queue.dma_start(
                     out=out_2[:, 4 * q : 4 * q + 4, first * P : last * P].bitcast(I32).rearrange("g r m -> r g m"),
                     in_=y_scales[first, last][32 * q : 32 * q + 4, :, :].bitcast(I32),
                 )
 
-        def quantize_y(s):
-            j, h = divmod(s, HALVES)
-            first, last = scale_spans[j >= EARLY_SCALE_TILES]
+        def quantize_tiles(unit, count, values):
+            j, h = divmod(unit, HALVES)
+            first, last = scale_spans[j >= EARLY_PLANE_TILES]
             if j % 2 == 0:
                 y_codes[h] = work.tile([P, 2 * P], U32, name="y_codes", tag="y_codes", bufs=6, align_bytes=64)
             col = (j % 2) * P
             nc.vector.quantize_mx(
-                out=y_codes[h][:, col : col + P].bitcast(FP8X4),
-                scales=y_scales[first, last][:, h, (j - first) * P : (j - first + 1) * P],
-                in_=y_turned[s],
+                out=y_codes[h][:, col : col + count * P].bitcast(FP8X4),
+                scales=y_scales[first, last][:, h, (j - first) * P : (j - first + count) * P],
+                in_=values,
             )
-            if j % 2 == 1:
+            newest = j + count - 1
+            if newest % 2 == 1:
                 nc.sync.dma_start(
-                    out=out_1[h].rearrange("p m t -> p (m t)")[:, (j - 1) * 4 * P : (j + 1) * 4 * P].bitcast(I32),
+                    out=out_1[h]
+                    .rearrange("p m t -> p (m t)")[:, (newest - 1) * 4 * P : (newest + 1) * 4 * P]
+                    .bitcast(I32),
                     in_=y_codes[h][:].bitcast(I32),
                 )
-            if h == HALVES - 1 and j == last - 1:
+            if h == HALVES - 1 and newest == last - 1:
                 store_scales(first, last)
 
-        def quantize_group(units):
-            for s in units:
-                quantize_y(s)
-
-        FIRST, REST = (0, 1), (2,)
-        LAST = UNITS - 1
-        ALL = slice(0, N)
-
-        def half(u):
-            return u // HALVES, slice((u % HALVES) * HALF, (u % HALVES + 1) * HALF)
-
-        order = [0, 2, 1, 3] + list(range(4, UNITS))
-        halves_done, wholes_done = {}, {}
-        for s, u in enumerate(order):
-            if WHOLE_FROM <= u // HALVES < SPLIT:
-                if u % HALVES == 1:
-                    wholes_done[s] = u // HALVES
+        def quantize_y(group):
+            if len(group) == 2 and group[1] == group[0] + HALVES and group[0] // HALVES % 2 == 0:
+                quantize_tiles(group[0], 2, y_turned[group][:])
             else:
-                halves_done[s] = u
+                for i, unit in enumerate(group):
+                    quantize_tiles(unit, 1, y_turned[group][:, i * PASS : (i + 1) * PASS])
 
-        warm_up(WARM1)
+        def columns(unit):
+            j, h = divmod(unit, HALVES)
+            return j, slice(h * PASS, (h + 1) * PASS)
+
+        whole = slice(0, N)
+        last_step = UNITS - 1
+        order = [0, 2, 1, 3] + list(range(4, UNITS))
+        unit_done, tile_done = {}, {}
+        for step, unit in enumerate(order):
+            if not WHOLE_FROM <= unit // HALVES < WHOLE_TO:
+                unit_done[step] = unit
+            elif unit % HALVES == HALVES - 1:
+                tile_done[step] = unit // HALVES
+
+        warm_up(WARM_UP[0])
         for g in range(PASSES):
             widen(0, g)
-            turn_x(0, (g,))
-            copy_x(0, (g,))
-        warm_up(WARM2)
+            turn_x(((0, g),))
+            copy_x(((0, g),))
+        warm_up(WARM_UP[1])
         for g in range(PASSES):
             widen(1, g)
-            quantize_x(0, (g,))
+            quantize_x(((0, g),))
         for g in range(PASSES):
             widen(2, g)
-        for passes in (FIRST, REST):
-            turn_x(1, passes)
-            copy_x(1, passes)
-        multiply(0, 0)
-        square(0, 0, half(0)[1])
-        for passes in (FIRST, REST):
-            quantize_x(1, passes)
-        to_turn = list(range(HEAD_TURN, TILES))
-        to_copy = []
-        if HEAD_TURN == 3:
-            for passes in (FIRST, REST):
-                turn_x(2, passes)
-            to_copy.append(2)
+        for batch in x_batches(1):
+            turn_x(batch)
+            copy_x(batch)
+        multiply(order[0], 0)
+        square(*columns(order[0]), 0)
+        for batch in x_batches(1):
+            quantize_x(batch)
         spread_thr()
-        if I_FIRST:
-            multiply(order[1], 0)
-        multiply(0, 1)
+        multiply(order[0], 1)
+
         to_widen = [(j, g) for j in range(3, TILES) for g in range(PASSES)]
-        late_head = to_widen[: (HEAD_WIDE - 3) * PASSES]
-        to_widen = to_widen[(HEAD_WIDE - 3) * PASSES :]
-
-        narrowed, y_groups = [], []
-        for s, u in enumerate(order):
-            step_tile, h = divmod(s, HALVES)
-            j, cols = half(u)
-            if s > I_FIRST:
-                multiply(u, 0)
-            if s > 0:
-                multiply(u, 1)
-            turned = to_copy[:1]
-            to_copy = to_copy[1:]
-            for tile in turned:
-                copy_x(tile, FIRST)
-                copy_x(tile, REST)
-            copied = ()
-            if y_groups and h != Y_EVEN:
-                copied = y_groups[0]
-                y_groups = y_groups[1:]
-                copy_y(copied)
-            if s > 0:
-                square(j, 0, cols)
-            if s == 0:
-                for tile, g in late_head:
-                    widen(tile, g)
-            if s - 2 in halves_done:
-                subtract(*half(halves_done[s - 2]))
-            if s - 1 in wholes_done:
-                add(wholes_done[s - 1], ALL)
-                root(wholes_done[s - 1], ALL)
-            if s - 1 in halves_done:
-                add(*half(halves_done[s - 1]))
-                if s < LAST:
-                    root(*half(halves_done[s - 1]))
-            if s < LAST:
-                square(j, 1, cols)
-            if s - 3 in wholes_done:
-                tile = wholes_done[s - 3]
-                narrow(tile, ALL)
-                narrowed.extend([(s, HALVES * tile), (s, HALVES * tile + 1)])
-            if s - 2 in halves_done:
-                narrow(*half(halves_done[s - 2]))
-                narrowed.append((s, halves_done[s - 2]))
-            for tile in turned:
-                quantize_x(tile, FIRST)
-                quantize_x(tile, REST)
-            count = WIDENS[h]
-            for tile, g in to_widen[:count]:
-                widen(tile, g)
-            to_widen = to_widen[count:]
-            quantize_group(copied)
-            if s - 2 in wholes_done:
-                subtract(wholes_done[s - 2], ALL)
-            if h == 1:
-                count = 2 if step_tile < DOUBLE_RUNS else 1
-                for tile in to_turn[:count]:
-                    turn_x(tile, FIRST)
-                    turn_x(tile, REST)
-                    to_copy.append(tile)
-                to_turn = to_turn[count:]
-                group = tuple(unit for when, unit in narrowed if when <= s - Y_LAG)[:2]
-                if group and s < LAST:
+        x_waiting, narrowed, y_waiting = [], [], []
+        for step, unit in enumerate(order):
+            if step > 0:
+                multiply(unit, 0)
+                multiply(unit, 1)
+            x_now, x_waiting = x_waiting, []
+            y_now, y_waiting = y_waiting, []
+            for batch in x_now:
+                copy_x(batch)
+            for group in y_now:
+                copy_y(group)
+            if step > 0:
+                square(*columns(unit), 0)
+            if step - 2 in unit_done:
+                subtract(*columns(unit_done[step - 2]))
+            if step - 1 in tile_done:
+                add(tile_done[step - 1], whole)
+                root(tile_done[step - 1], whole)
+            if step - 1 in unit_done:
+                add(*columns(unit_done[step - 1]))
+                if step < last_step:
+                    root(*columns(unit_done[step - 1]))
+            if step < last_step:
+                square(*columns(unit), 1)
+            if step - 3 in tile_done:
+                j = tile_done[step - 3]
+                narrow(j, whole)
+                if j % 2 == 1:
+                    narrowed.extend([(step, HALVES * i + h) for h in range(HALVES) for i in (j - 1, j)])
+            if step - 2 in unit_done:
+                narrow(*columns(unit_done[step - 2]))
+                narrowed.append((step, unit_done[step - 2]))
+            for batch in x_now:
+                quantize_x(batch)
+            for j, g in to_widen[:WIDEN_PER_STEP]:
+                widen(j, g)
+            to_widen = to_widen[WIDEN_PER_STEP:]
+            for group in y_now:
+                quantize_y(group)
+            if step - 2 in tile_done:
+                subtract(tile_done[step - 2], whole)
+            if step % 2 == 1:
+                if step // 2 + 2 < TILES:
+                    x_waiting = x_batches(step // 2 + 2)
+                    for batch in x_waiting:
+                        turn_x(batch)
+                group = tuple(ready for when, ready in narrowed if when < step)[:2]
+                if len(group) == 2 and step < last_step:
                     turn_y(group)
-                    y_groups.append(group)
-                    narrowed = narrowed[len(group) :]
+                    y_waiting = [group]
+                    narrowed = narrowed[2:]
 
-        width = HALF // PIECES
-        pieces = [slice(c, c + width) for c in range(HALF, N, width)]
+        width = PASS // LAST_PIECES
+        pieces = [slice(c, c + width) for c in range(N - PASS, N, width)]
         j = TILES - 1
-        waiting = [u for when, u in narrowed]
-        for i in range(0, len(waiting), 2):
-            group = tuple(waiting[i : i + 2])
+        before_last, last_unit = UNITS - 2, UNITS - 1
+        left = [ready for when, ready in narrowed]
+        left_groups = [tuple(left[i : i + 2]) for i in range(0, len(left), 2)]
+        for group in left_groups:
             turn_y(group)
-            y_groups.append(group)
-        for c in pieces:
-            square(j, 1, c)
-        root(*half(LAST - 1))
-        for c in pieces:
-            add(j, c)
-            root(j, c)
-        subtract(*half(LAST - 1))
-        for group in y_groups:
+        for cols in pieces:
+            square(j, cols, 1)
+        root(*columns(before_last))
+        for cols in pieces:
+            add(j, cols)
+            root(j, cols)
+        subtract(*columns(before_last))
+        for group in left_groups:
             copy_y(group)
         subtract(j, pieces[0])
-        narrow(*half(LAST - 1))
-        turn_y((LAST - 1,))
-        copy_y((LAST - 1,))
-        for c in pieces[1:]:
-            subtract(j, c)
-        for c in pieces:
-            narrow(j, c)
-        turn_y((LAST,))
-        copy_y((LAST,))
-        for group in y_groups:
-            quantize_group(group)
-        quantize_y(LAST - 1)
-        quantize_y(LAST)
+        narrow(*columns(before_last))
+        turn_y((before_last,))
+        copy_y((before_last,))
+        for cols in pieces[1:]:
+            subtract(j, cols)
+        for cols in pieces:
+            narrow(j, cols)
+        turn_y((last_unit,))
+        copy_y((last_unit,))
+        for group in left_groups + [(before_last,), (last_unit,)]:
+            quantize_y(group)

from contextlib import ExitStack

import concourse.mybir as mybir
from concourse.masks import make_identity

T, K, N = 1280, 1536, 1024
FLOPS = 2 * 2 * T * K * N

F32 = mybir.dt.float32
BF16 = mybir.dt.bfloat16
I32 = mybir.dt.int32
U32 = mybir.dt.uint32
U8 = mybir.dt.uint8
FP8 = mybir.dt.float8_e4m3fn
FP8X4 = mybir.dt.float8_e4m3fn_x4
FP4X4 = mybir.dt.float4_e2m1fn_x4
ALU = mybir.AluOpType
ACT = mybir.ActivationFunctionType

P = 128
PASS = 512
PASSES = K // PASS
HALVES = N // PASS
TILES = T // P
UNITS = TILES * HALVES
STORED_BLOCK = 128
STORED_BLOCKS = K // STORED_BLOCK
STORED_PITCH = 16
QUADRANTS = 4

BANKS = 8
PRODUCT_BANKS = 4
X_LOADS = ((0, 1), (1, 3), (3, 5), (5, 7), (7, 10))
EARLY_SCALE_LOAD = 5
WHOLE_FROM, WHOLE_TO = 2, 8
WIDEN_PER_STEP = 2
VECTOR_COPIES_FROM = 7
LAST_PIECES = 2
EARLY_PLANE_TILES = 6
WARM_UP = (14, 8)


def tile_radar_iq_envelope_planes_b2_kernel(
    tc, X_bytes, X_scale, Wi_words, Wi_scales, Wq_words, Wq_scales, thr, out_0, out_1, out_2
):
    nc = tc.nc
    with ExitStack() as ctx:
        keep = ctx.enter_context(tc.tile_pool(name="keep", bufs=1))
        work = ctx.enter_context(tc.tile_pool(name="work", bufs=3))
        psum = ctx.enter_context(tc.psum_pool(name="psum", bufs=1))
        ctx.enter_context(tc.manual_schedule())

        free_banks = {"product": list(range(PRODUCT_BANKS)), "turn": list(range(PRODUCT_BANKS, BANKS))}
        bank_of = {}

        def next_bank(role, key):
            number = free_banks[role][0]
            free_banks[role].remove(number)
            bank_of[key] = (role, number)
            return psum.tile([P, PASS], F32, name="bank%d" % number, tag="bank%d" % number)

        def emptied(key):
            role, number = bank_of[key]
            free_banks[role].append(number)

        ident = keep.tile([P, P], F32, name="ident")
        make_identity(nc, ident[:])
        table_probe = keep.tile([P, 2], F32, name="table_probe")
        w_scales = []
        for name in ("wi_scales", "wq_scales"):
            scale_tile = keep.tile([P, PASSES * N], U8, name=name, align_bytes=64)
            w_scales.append(scale_tile)
        idle_values = keep.tile([P, PASS], BF16, name="idle_values", align_bytes=64)
        idle_codes = keep.tile([P, P], U32, name="idle_codes", align_bytes=64)
        idle_scales = keep.tile([P, P], U8, name="idle_scales", align_bytes=64)
        nc.vector.memset(idle_values[:].bitcast(I32), 0)
        nc.vector.memset(w_scales[0][:].bitcast(I32), 0)
        nc.vector.quantize_mx(out=idle_codes[:].bitcast(FP8X4), scales=idle_scales[:], in_=idle_values[:])
        nc.vector.memset(table_probe[:, 0:1], 1.0)
        nc.vector.memset(w_scales[1][:].bitcast(I32), 0)
        nc.scalar.activation(out=table_probe[:, 1:2], in_=table_probe[:, 0:1], func=ACT.Sqrt)

        def warm_up(count):
            bank = next_bank("product", "idle")
            for i in range(count):
                col = (i % (PASS // P)) * P
                nc.tensor.matmul_mx(
                    out=bank[:, col : col + P],
                    lhsT=idle_codes[:].bitcast(FP8X4),
                    lhsT_scale=idle_scales[:],
                    rhs=idle_codes[:, : P // 2].bitcast(FP4X4),
                    rhs_scale=idle_scales[:],
                    start=True,
                    stop=True,
                )
            emptied("idle")

        x_raw, x_stored_scale, w_words = {}, {}, {}

        def load_x(first, last):
            raw = keep.tile([P, last - first, K], U8, name="x_raw%d" % first)
            nc.sync.dma_start(out=raw[:], in_=X_bytes[first * P : last * P, :].rearrange("(j p) k -> p j k", p=P))
            for j in range(first, last):
                x_raw[j] = raw[:, j - first, :]

        def load_x_scales(first, last):
            rows = keep.tile([P, last - first, STORED_PITCH], F32, name="x_stored_scale%d" % first)
            nc.sync.dma_start(
                out=rows[:, :, :STORED_BLOCKS],
                in_=X_scale[first * P : last * P, :].rearrange("(j p) c -> p j c", p=P),
            )
            for j in range(first, last):
                x_stored_scale[j] = rows[:, j - first, :]

        def load_w_scales(part):
            src = (Wi_scales, Wq_scales)[part]
            for r in range(4):
                nc.sync.dma_start(
                    out=w_scales[part][r:P:32, :].bitcast(I32).rearrange("q (g n) -> q g n", g=PASSES),
                    in_=src[:, r:16:4, :].bitcast(I32).rearrange("g q n -> q g n"),
                )

        def load_w_words(part, h):
            src = (Wi_words, Wq_words)[part]
            words = keep.tile([P, PASSES, 2 * PASS], U8, name="w_words%d%d" % (part, h), align_bytes=64)
            nc.sync.dma_start(
                out=words[:], in_=src[:, :, 2 * PASS * h : 2 * PASS * (h + 1)].rearrange("g p b -> p g b")
            )
            w_words[part, h] = words

        load_x(*X_LOADS[0])
        load_x_scales(0, EARLY_SCALE_LOAD)
        load_x(*X_LOADS[1])
        load_w_scales(0)
        load_w_words(0, 0)
        thr_words = keep.tile([P, N // P], BF16, name="thr_words")
        nc.sync.dma_start(out=thr_words[:], in_=thr.rearrange("o (p c) -> p (o c)", p=P))
        load_w_scales(1)
        load_w_words(1, 0)
        load_x(*X_LOADS[2])
        load_w_words(0, 1)
        load_w_words(1, 1)
        load_x_scales(EARLY_SCALE_LOAD, TILES)
        load_x(*X_LOADS[3])
        load_x(*X_LOADS[4])

        thr_rows = keep.tile([P, N], BF16, name="thr_rows")

        def spread_thr():
            bank = next_bank("turn", "thr")
            words = thr_words[:].bitcast(F32)
            for c in range(4):
                nc.tensor.transpose(bank[:, c * P : (c + 1) * P], words[:, c : c + 1].to_broadcast([P, P]), ident[:])
            nc.scalar.copy(
                out=thr_rows[:].bitcast(F32).rearrange("p (j c) -> p j c", c=4),
                in_=bank[:].rearrange("p (c j) -> p j c", c=4),
            )
            emptied("thr")

        x_wide, x_bank, x_turned, x_codes, x_scales = {}, {}, {}, {}, {}

        def widen(j, g):
            wide = work.tile([P, PASS], BF16, name="x_wide", tag="x_wide", bufs=15)
            for q in range(PASS // STORED_BLOCK):
                b = (PASS // STORED_BLOCK) * g + q
                nc.vector.tensor_scalar(
                    out=wide[:, STORED_BLOCK * q : STORED_BLOCK * (q + 1)],
                    in0=x_raw[j][:, STORED_BLOCK * b : STORED_BLOCK * (b + 1)].bitcast(FP8),
                    scalar1=x_stored_scale[j][:, b : b + 1],
                    scalar2=None,
                    op0=ALU.mult,
                )
            x_wide[j, g] = wide

        def turn_x(batch):
            bank = next_bank("turn", ("x", batch))
            for i, key in enumerate(batch):
                words = x_wide[key][:].bitcast(F32)
                for u in range(2):
                    col = (2 * i + u) * P
                    nc.tensor.transpose(bank[:, col : col + P], words[:, u : 2 * P : 2], ident[:])
            x_bank[batch] = bank

        def copy_x(batch):
            count = len(batch)
            turned = work.tile([P, count * PASS], BF16, name="x_turned", tag="x_turned", bufs=6, align_bytes=64)
            on_vector = count == 2 and batch[0][0] >= VECTOR_COPIES_FROM
            copy = nc.vector.tensor_copy if on_vector else nc.scalar.copy
            copy(
                out=turned[:].bitcast(F32).rearrange("p (g m u) -> p g m u", g=count, u=2),
                in_=x_bank[batch][:, : count * 2 * P].rearrange("p (g u m) -> p g m u", g=count, u=2),
            )
            x_turned[batch] = turned
            emptied(("x", batch))

        def quantize_x(batch):
            count = len(batch)
            codes = work.tile([P, count * P], U32, name="x_codes", tag="x_codes", bufs=16, align_bytes=64)
            scales = work.tile([P, count * P], U8, name="x_scales", tag="x_scales", bufs=16, align_bytes=64)
            nc.vector.quantize_mx(out=codes[:].bitcast(FP8X4), scales=scales[:], in_=x_turned[batch][:])
            for i, key in enumerate(batch):
                x_codes[key] = codes[:, i * P : (i + 1) * P]
                x_scales[key] = scales[:, i * P : (i + 1) * P]

        def x_batches(j):
            return [((j, 0), (j, 1)), ((j, 2),)]

        product, squares, power, envelope, y, y_narrow = {}, {}, {}, {}, {}, {}

        def multiply(unit, part):
            j, h = divmod(unit, HALVES)
            bank = next_bank("product", ("product", unit, part))
            for g in range(PASSES):
                nc.tensor.matmul_mx(
                    out=bank[:],
                    lhsT=x_codes[j, g].bitcast(FP8X4),
                    lhsT_scale=x_scales[j, g],
                    rhs=w_words[part, h][:, g, :].bitcast(FP4X4),
                    rhs_scale=w_scales[part][:, g * N + h * PASS : g * N + (h + 1) * PASS],
                    start=(g == 0),
                    stop=(g == PASSES - 1),
                )
            product[unit, part] = bank

        def square(j, cols, part):
            if cols.start == 0:
                squares[j, part] = work.tile([P, N], F32, name="square", tag="square", bufs=5)
            h = cols.start // PASS
            unit = HALVES * j + h
            nc.scalar.activation(
                out=squares[j, part][:, cols],
                in_=product[unit, part][:, cols.start - h * PASS : cols.stop - h * PASS],
                func=ACT.Square,
            )
            if cols.stop % PASS == 0:
                emptied(("product", unit, part))

        def add(j, cols):
            if cols.start == 0:
                power[j] = work.tile([P, N], F32, name="power", tag="power", bufs=3)
            nc.vector.tensor_tensor(
                out=power[j][:, cols], in0=squares[j, 0][:, cols], in1=squares[j, 1][:, cols], op=ALU.add
            )

        def root(j, cols):
            if cols.start == 0:
                envelope[j] = work.tile([P, N], F32, name="envelope", tag="envelope", bufs=3)
            nc.scalar.activation(out=envelope[j][:, cols], in_=power[j][:, cols], func=ACT.Sqrt)

        def subtract(j, cols):
            if cols.start == 0:
                y[j] = work.tile([P, N], F32, name="y", tag="y", bufs=4)
            nc.vector.tensor_tensor(out=y[j][:, cols], in0=envelope[j][:, cols], in1=thr_rows[:, cols], op=ALU.subtract)
            if cols.stop % PASS == 0:
                stored = slice(min(cols.start, cols.stop - PASS), cols.stop)
                nc.sync.dma_start(out=out_0[j * P : (j + 1) * P, stored], in_=y[j][:, stored])

        def narrow(j, cols):
            if cols.start == 0:
                y_narrow[j] = work.tile([P, N], BF16, name="y_narrow", tag="y_narrow", bufs=5)
            sorted_view = y_narrow[j][:].rearrange("p (h u r e) -> p h u r e", h=HALVES, u=2, e=2)
            if cols.stop - cols.start == N:
                nc.vector.tensor_copy(
                    out=sorted_view, in_=y[j][:].rearrange("p (h r u e) -> p h u r e", h=HALVES, u=2, e=2)
                )
            else:
                h = cols.start // PASS
                rows = slice((cols.start - h * PASS) // 4, (cols.stop - h * PASS) // 4)
                nc.vector.tensor_copy(
                    out=sorted_view[:, h, :, rows, :], in_=y[j][:, cols].rearrange("p (r u e) -> p u r e", u=2, e=2)
                )

        y_bank, y_turned, y_codes, y_scales = {}, {}, {}, {}
        scale_spans = ((0, EARLY_PLANE_TILES), (EARLY_PLANE_TILES, TILES))
        for first, last in scale_spans:
            y_scales[first, last] = keep.tile(
                [P, HALVES, (last - first) * P], U8, name="y_scales%d" % first, align_bytes=64
            )

        def turn_y(group):
            bank = next_bank("turn", ("y", group))
            for i, unit in enumerate(group):
                j, h = divmod(unit, HALVES)
                words = y_narrow[j][:, h * PASS : (h + 1) * PASS].bitcast(F32)
                for u in range(2):
                    col = (2 * i + u) * P
                    nc.tensor.transpose(bank[:, col : col + P], words[:, u * P : (u + 1) * P], ident[:])
            y_bank[group] = bank

        def copy_y(group):
            count = len(group)
            turned = work.tile([P, count * PASS], BF16, name="y_turned", tag="y_turned", bufs=5, align_bytes=64)
            nc.scalar.copy(
                out=turned[:].bitcast(F32).rearrange("p (g m u) -> p g m u", g=count, u=2),
                in_=y_bank[group][:, : count * 2 * P].rearrange("p (g u m) -> p g m u", g=count, u=2),
            )
            emptied(("y", group))
            y_turned[group] = turned

        def store_scales(first, last):
            for i, q in enumerate((0, 2, 1, 3)):
                queue = nc.scalar if last == TILES and i < QUADRANTS // 2 else nc.sync
                queue.dma_start(
                    out=out_2[:, 4 * q : 4 * q + 4, first * P : last * P].bitcast(I32).rearrange("g r m -> r g m"),
                    in_=y_scales[first, last][32 * q : 32 * q + 4, :, :].bitcast(I32),
                )

        def quantize_tiles(unit, count, values):
            j, h = divmod(unit, HALVES)
            first, last = scale_spans[j >= EARLY_PLANE_TILES]
            if j % 2 == 0:
                y_codes[h] = work.tile([P, 2 * P], U32, name="y_codes", tag="y_codes", bufs=6, align_bytes=64)
            col = (j % 2) * P
            nc.vector.quantize_mx(
                out=y_codes[h][:, col : col + count * P].bitcast(FP8X4),
                scales=y_scales[first, last][:, h, (j - first) * P : (j - first + count) * P],
                in_=values,
            )
            newest = j + count - 1
            if newest % 2 == 1:
                nc.sync.dma_start(
                    out=out_1[h]
                    .rearrange("p m t -> p (m t)")[:, (newest - 1) * 4 * P : (newest + 1) * 4 * P]
                    .bitcast(I32),
                    in_=y_codes[h][:].bitcast(I32),
                )
            if h == HALVES - 1 and newest == last - 1:
                store_scales(first, last)

        def quantize_y(group):
            if len(group) == 2 and group[1] == group[0] + HALVES and group[0] // HALVES % 2 == 0:
                quantize_tiles(group[0], 2, y_turned[group][:])
            else:
                for i, unit in enumerate(group):
                    quantize_tiles(unit, 1, y_turned[group][:, i * PASS : (i + 1) * PASS])

        def columns(unit):
            j, h = divmod(unit, HALVES)
            return j, slice(h * PASS, (h + 1) * PASS)

        whole = slice(0, N)
        last_step = UNITS - 1
        order = [0, 2, 1, 3] + list(range(4, UNITS))
        unit_done, tile_done = {}, {}
        for step, unit in enumerate(order):
            if not WHOLE_FROM <= unit // HALVES < WHOLE_TO:
                unit_done[step] = unit
            elif unit % HALVES == HALVES - 1:
                tile_done[step] = unit // HALVES

        warm_up(WARM_UP[0])
        for g in range(PASSES):
            widen(0, g)
            turn_x(((0, g),))
            copy_x(((0, g),))
        warm_up(WARM_UP[1])
        for g in range(PASSES):
            widen(1, g)
            quantize_x(((0, g),))
        for g in range(PASSES):
            widen(2, g)
        for batch in x_batches(1):
            turn_x(batch)
            copy_x(batch)
        multiply(order[0], 0)
        square(*columns(order[0]), 0)
        for batch in x_batches(1):
            quantize_x(batch)
        spread_thr()
        multiply(order[0], 1)

        to_widen = [(j, g) for j in range(3, TILES) for g in range(PASSES)]
        x_waiting, narrowed, y_waiting = [], [], []
        for step, unit in enumerate(order):
            if step > 0:
                multiply(unit, 0)
                multiply(unit, 1)
            x_now, x_waiting = x_waiting, []
            y_now, y_waiting = y_waiting, []
            for batch in x_now:
                copy_x(batch)
            for group in y_now:
                copy_y(group)
            if step > 0:
                square(*columns(unit), 0)
            if step - 2 in unit_done:
                subtract(*columns(unit_done[step - 2]))
            if step - 1 in tile_done:
                add(tile_done[step - 1], whole)
                root(tile_done[step - 1], whole)
            if step - 1 in unit_done:
                add(*columns(unit_done[step - 1]))
                if step < last_step:
                    root(*columns(unit_done[step - 1]))
            if step < last_step:
                square(*columns(unit), 1)
            if step - 3 in tile_done:
                j = tile_done[step - 3]
                narrow(j, whole)
                if j % 2 == 1:
                    narrowed.extend([(step, HALVES * i + h) for h in range(HALVES) for i in (j - 1, j)])
            if step - 2 in unit_done:
                narrow(*columns(unit_done[step - 2]))
                narrowed.append((step, unit_done[step - 2]))
            for batch in x_now:
                quantize_x(batch)
            for j, g in to_widen[:WIDEN_PER_STEP]:
                widen(j, g)
            to_widen = to_widen[WIDEN_PER_STEP:]
            for group in y_now:
                quantize_y(group)
            if step - 2 in tile_done:
                subtract(tile_done[step - 2], whole)
            if step % 2 == 1:
                if step // 2 + 2 < TILES:
                    x_waiting = x_batches(step // 2 + 2)
                    for batch in x_waiting:
                        turn_x(batch)
                group = tuple(ready for when, ready in narrowed if when < step)[:2]
                if len(group) == 2 and step < last_step:
                    turn_y(group)
                    y_waiting = [group]
                    narrowed = narrowed[2:]

        width = PASS // LAST_PIECES
        pieces = [slice(c, c + width) for c in range(N - PASS, N, width)]
        j = TILES - 1
        before_last, last_unit = UNITS - 2, UNITS - 1
        left = [ready for when, ready in narrowed]
        left_groups = [tuple(left[i : i + 2]) for i in range(0, len(left), 2)]
        for group in left_groups:
            turn_y(group)
        for cols in pieces:
            square(j, cols, 1)
        root(*columns(before_last))
        for cols in pieces:
            add(j, cols)
            root(j, cols)
        subtract(*columns(before_last))
        for group in left_groups:
            copy_y(group)
        subtract(j, pieces[0])
        narrow(*columns(before_last))
        turn_y((before_last,))
        copy_y((before_last,))
        for cols in pieces[1:]:
            subtract(j, cols)
        for cols in pieces:
            narrow(j, cols)
        turn_y((last_unit,))
        copy_y((last_unit,))
        for group in left_groups + [(before_last,), (last_unit,)]:
            quantize_y(group)
